import numpy as np
import ml_dtypes


def mxq(x, axis, fmt="e4m3"):
    dtype, down = {"e4m3": (ml_dtypes.float8_e4m3fn, 7), "e5m2": (ml_dtypes.float8_e5m2, 14)}[fmt]
    v = np.moveaxis(np.asarray(x, np.float32).astype(ml_dtypes.bfloat16).astype(np.float64), axis, -1)
    blocks = v.reshape(v.shape[:-1] + (-1, 32))
    amax = np.abs(blocks).max(-1, keepdims=True)
    byte = np.maximum(np.where(amax > 0, np.frexp(amax)[1] - 1 + 127, 0) - down, 1)
    scale = np.exp2(byte - 127.0)
    codes = (blocks / scale).astype(np.float32).astype(dtype).astype(np.float64)
    return np.moveaxis((codes * scale).reshape(v.shape), -1, axis)


WIDE = False


def mx_kscale(k):
    if not WIDE:
        return np.ones(k)
    levels = np.array([10, -10, 5, -5, 0])
    if k % 512:
        return np.exp2(np.random.permutation(np.resize(levels, k // 32))).repeat(32)
    a = np.empty((k // 512, 16))
    for p in range(k // 512):
        a[p, :8] = np.random.permutation(np.resize(levels, 8))
        for g in range(8):
            far = levels[np.abs(levels - a[p, g]) >= 10]
            a[p, g + 8] = far[np.random.randint(len(far))]
    return np.exp2(a.ravel()).repeat(32)


def f64(x):
    return np.asarray(x).astype(np.float64)


def striped(idx):
    return np.tile(idx.reshape(-1, 16).T, (8, 1)).astype(np.uint16)


def unstriped(offs):
    return offs[:16].T.reshape(-1).astype(np.int64)


E2M1 = np.array([0.0, 0.5, 1.0, 1.5, 2.0, 3.0, 4.0, 6.0, -0.0, -0.5, -1.0, -1.5, -2.0, -3.0, -4.0, -6.0])


def pack_weight(w, fmt):
    k, n = w.shape
    w = f64(np.asarray(w, np.float32).astype(ml_dtypes.bfloat16)).reshape(k // 32, 32, n)
    amax = np.abs(w).max(1)
    if fmt == "e4m3":
        byte = np.frexp(amax)[1] - 1 + 127 - 7
    else:
        mant, ex = np.frexp(amax / 6.0)
        byte = np.where(mant > 0.5, ex, ex - 1) + 127
    byte = np.clip(np.where(amax > 0, byte, 1), 1, 254)
    scaled = (w * np.exp2(127.0 - byte)[:, None, :]).reshape(k, n).astype(np.float32)
    by_word = np.ascontiguousarray(scaled.reshape(k // 512, 128, 4, n).transpose(0, 1, 3, 2))
    if fmt == "e4m3":
        words = by_word.astype(ml_dtypes.float8_e4m3fn).view(np.uint8)
    else:
        c = by_word.astype(ml_dtypes.float4_e2m1fn).view(np.uint8) & 0xF
        words = (c[..., 0::2] | (c[..., 1::2] << 4)).reshape(k // 512, 128, 2 * n)
    return np.ascontiguousarray(words), np.ascontiguousarray(byte.astype(np.uint8).reshape(k // 512, 16, n))


def unpack_weight(words, scales, fmt):
    g, _, n = scales.shape
    words = np.ascontiguousarray(words).reshape(g, 128, n, -1)
    if fmt == "e4m3":
        vals = words.view(ml_dtypes.float8_e4m3fn).astype(np.float64)
    else:
        nib = np.empty((g, 128, n, 4), np.uint8)
        nib[..., 0::2] = words & 0xF
        nib[..., 1::2] = words >> 4
        vals = E2M1[nib]
    vals = vals * np.repeat(np.exp2(scales.astype(np.float64) - 127.0), 8, axis=1)[..., None]
    return vals.transpose(0, 1, 3, 2).reshape(g * 512, n)


def silu(v):
    return v / (1.0 + np.exp(-np.maximum(v, -700.0)))


K, T, E, C, H, N = 1536, 640, 5, 256, 512, 128


def by_expert(wq, xq):
    return np.concatenate([wq[e].T @ xq[:, e * C:(e + 1) * C] for e in range(E)], axis=1)


def setup_inputs():
    n = np.random.standard_normal
    s = mx_kscale(K)[:, None]
    u = mx_kscale(H)
    first = np.random.permutation(np.repeat(np.arange(E), T // E))
    second = (first + 1 + np.random.permutation(np.repeat(np.arange(E - 1), -(-T // (E - 1)))[:T])) % E
    while np.bincount(second, minlength=E).max() != T // E:
        load = np.bincount(second, minlength=E); hi, lo = int(load.argmax()), int(load.argmin())
        t = np.flatnonzero((second == hi) & (first != lo))[0]; second[t] = lo
    slot_token = np.empty(E * C, np.int64); pos = np.empty((2, T), np.int64); fill = np.zeros(E, np.int64)
    place = np.stack([np.random.permutation(C) for _ in range(E)])
    for r, deal in enumerate((first, second)):
        for t in np.random.permutation(T):
            e = deal[t]; j = e * C + place[e, fill[e]]; fill[e] += 1; slot_token[j] = t; pos[r, t] = j
    g = np.random.uniform(0.2, 0.8, T)
    w1 = [pack_weight(m, "e2m1") for m in n((E, K, H)) / np.sqrt(K) / s[None] * u[None, None, :]]
    w2 = [pack_weight(m, "e2m1") for m in n((E, H, N)) / np.sqrt(H) / u[None, :, None]]
    w_slot = np.empty(E * C); w_slot[pos[0]] = g; w_slot[pos[1]] = 1.0 - g
    return {
        "xT": (n((K, T)) * s).astype(np.float32),
        "w1_words": np.stack([m[0] for m in w1]),
        "w1_scales": np.stack([m[1] for m in w1]),
        "w2_words": np.stack([m[0] for m in w2]),
        "w2_scales": np.stack([m[1] for m in w2]),
        "gate": np.tile(w_slot, (K, 1)).astype(np.float32),
        "offs": striped(slot_token),
        "pos1": striped(pos[0]),
        "pos2": striped(pos[1]),
    }


def reference(xT, w1_words, w1_scales, w2_words, w2_scales, gate, offs, pos1, pos2):
    idx = unstriped(offs)
    w1 = np.stack([unpack_weight(w1_words[e], w1_scales[e], "e2m1") for e in range(E)])
    w2 = np.stack([unpack_weight(w2_words[e], w2_scales[e], "e2m1") for e in range(E)])
    xq = mxq(f64(gate) * f64(xT)[:, idx], 0, "e4m3")
    h = silu(by_expert(w1, xq))
    y = by_expert(w2, mxq(h, 0, "e4m3"))
    return y[:, unstriped(pos1)] + y[:, unstriped(pos2)]

@@ -1,0 +1,166 @@
+from contextlib import ExitStack
+
+import concourse.mybir as mybir
+from concourse.masks import make_identity
+
+K, T, E, C, H, N = 1536, 640, 5, 256, 512, 128
+S = E * C
+P = 128
+PACK = 4
+PASSES = K // (P * PACK)
+UNIT = 128
+GROUPS = [(0, 4), (4, 3), (7, 2), (9, 1)]
+OUT_PIECES = [(0, 384), (384, 256)]
+
+FLOPS = 2 * S * (K * H + H * N)
+BYTES = 4 * K * T + E * (K * H + H * N) // 2 + E * (K * H + H * N) // 32 + 4 * S + 2 * P * (S + 2 * T) // 16 + 4 * N * T
+
+F32 = mybir.dt.float32
+BF16 = mybir.dt.bfloat16
+I32 = mybir.dt.int32
+U32 = mybir.dt.uint32
+U16 = mybir.dt.uint16
+U8 = mybir.dt.uint8
+FP8X4 = mybir.dt.float8_e4m3fn_x4
+FP4X4 = mybir.dt.float4_e2m1fn_x4
+MULT = mybir.AluOpType.mult
+ADD = mybir.AluOpType.add
+SILU = mybir.ActivationFunctionType.Silu
+
+
+def chunks(units):
+    return [(a, min(2, units - a)) for a in range(0, units, 2)]
+
+
+def tile_moe_pre_mlp_silu_kernel(
+    tc, xT, w1_words, w1_scales, w2_words, w2_scales, gate, offs, pos1, pos2, out
+):
+    nc = tc.nc
+    with ExitStack() as ctx:
+        held = ctx.enter_context(tc.tile_pool(name="held", bufs=1))
+        ring = ctx.enter_context(tc.tile_pool(name="ring", bufs=3))
+        psum = ctx.enter_context(tc.psum_pool(name="psum", bufs=1))
+
+        offs_sb = held.tile([P, S // 16], U16, name="offs_sb")
+        pos1_sb = held.tile([P, T // 16], U16, name="pos1_sb")
+        pos2_sb = held.tile([P, T // 16], U16, name="pos2_sb")
+        x_rows = xT.rearrange("(s p j) t -> s j p t", p=P, j=PACK)
+        x_sb = {(s, j): held.tile([P, T], F32, name=f"x_{s}_{j}") for s in range(PASSES) for j in range(PACK)}
+        first = GROUPS[0][1] * UNIT
+        gate_a = held.tile([P, first], F32, name="gate_a")
+        gate_b = held.tile([P, S - first], F32, name="gate_b")
+        w1_sb = [held.tile([P, PASSES, 2 * H], U8, name=f"w1_{e}", align_bytes=64) for e in range(E)]
+        w2_sb = held.tile([P, E, 2 * N], U8, name="w2_sb", align_bytes=64)
+        w1_plane = held.tile([P, E * PASSES, H], U8, name="w1_plane", align_bytes=64)
+        w2_plane = held.tile([P, E, N], U8, name="w2_plane", align_bytes=64)
+        ident = held.tile([P, P], F32, name="ident")
+        y_sb = held.tile([P, S], F32, name="y_sb")
+
+        nc.vector.memset(w1_plane[:].rearrange("p a i -> p (a i)").bitcast(I32), 0)
+        nc.vector.memset(w2_plane[:].rearrange("p a i -> p (a i)").bitcast(I32), 0)
+        make_identity(nc, ident[:])
+
+        def load_x(s):
+            for j in range(PACK):
+                nc.sync.dma_start(x_sb[s, j][:], x_rows[s, j])
+
+        def load_w1(e):
+            nc.sync.dma_start(w1_sb[e][:].bitcast(I32), w1_words[e].rearrange("s p b -> p s b").bitcast(I32))
+
+        def load_plane(plane, scales, lo, hi):
+            rows = scales.rearrange("e s q i -> q (e s) i").bitcast(I32)
+            for quad in range(4):
+                nc.sync.dma_start(plane[32 * quad : 32 * quad + 4, lo:hi, :].bitcast(I32), rows[4 * quad : 4 * quad + 4, lo:hi, :])
+
+        nc.sync.dma_start(offs_sb[:], offs)
+        nc.sync.dma_start(gate_a[:], gate[0:P, 0:first])
+        load_x(0)
+        load_x(1)
+        load_plane(w1_plane, w1_scales, 0, 2 * PASSES)
+        load_w1(0)
+        load_x(2)
+        load_w1(1)
+        nc.sync.dma_start(gate_b[:], gate[0:P, first:S])
+        nc.sync.dma_start(w2_sb[:].bitcast(I32), w2_words.rearrange("e s p b -> p (e s) b").bitcast(I32))
+        load_plane(w1_plane, w1_scales, 2 * PASSES, E * PASSES)
+        load_plane(w2_plane, w2_scales, 0, E)
+        for e in range(2, E):
+            load_w1(e)
+        nc.sync.dma_start(pos1_sb[:], pos1)
+        nc.sync.dma_start(pos2_sb[:], pos2)
+
+        widest = max(units for u0, units in GROUPS) * UNIT
+        acc = {}
+
+        def first_layer(u0, units, s):
+            lo, n = u0 * UNIT, units * UNIT
+            gate_sb = gate_a[:, lo : lo + n] if lo < first else gate_b[:, lo - first : lo - first + n]
+            picked = ring.tile([P, PACK, widest], F32, name="picked")
+            for j in range(PACK):
+                window = x_sb[s, j][:].indirect(offs_sb[:, lo // 16 : (lo + n) // 16])
+                nc.vector.tensor_tensor(picked[:, j, 0:n], window, gate_sb, MULT)
+            grouped = ring.tile([P, widest, PACK], BF16, name="grouped", align_bytes=64)
+            codes = ring.tile([P, widest], U32, name="codes", align_bytes=64)
+            scales = ring.tile([P, widest], U8, name="scales", align_bytes=64)
+            for a, m in chunks(units):
+                cols = slice(a * UNIT, (a + m) * UNIT)
+                nc.scalar.copy(
+                    grouped[:, cols, :].rearrange("p (c i) t -> p c t i", i=4),
+                    picked[:, :, cols].rearrange("p t (c i) -> p c t i", i=4),
+                )
+                nc.vector.quantize_mx(codes[:, cols].bitcast(FP8X4), scales[:, cols], grouped[:, cols, :].rearrange("p c t -> p (c t)"))
+                for b in range(a, a + m):
+                    u = u0 + b
+                    e = u * UNIT // C
+                    if s == 0:
+                        acc[u] = psum.tile([P, H], F32, name="acc", bufs=5)
+                    one = slice(b * UNIT, (b + 1) * UNIT)
+                    nc.tensor.matmul_mx(
+                        out=acc[u][:],
+                        lhsT=codes[:, one].bitcast(FP8X4),
+                        lhsT_scale=scales[:, one],
+                        rhs=w1_sb[e][:, s, :].bitcast(FP4X4),
+                        rhs_scale=w1_plane[:, e * PASSES + s, :],
+                        start=(s == 0),
+                        stop=(s == PASSES - 1),
+                    )
+
+        def second_layer(u):
+            e = u * UNIT // C
+            hidden = ring.tile([P, 2, P, 2], BF16, name="hidden")
+            nc.scalar.activation(hidden[:], acc[u][:].rearrange("c (p v d) -> c v p d", v=2, d=2), SILU)
+            pairs = hidden[:].rearrange("c v p d -> c (v p d)").bitcast(F32)
+            turned = psum.tile([P, 2, UNIT], F32, name="turned", bufs=2)
+            for v in range(2):
+                nc.tensor.transpose(turned[:, v, :], pairs[:, v * P : (v + 1) * P], ident[:])
+            h_grouped = ring.tile([P, UNIT * PACK], BF16, name="h_grouped", align_bytes=64)
+            nc.scalar.copy(h_grouped[:].bitcast(F32).rearrange("p (c v) -> p c v", v=2), turned[:].rearrange("p v c -> p c v"))
+            h_codes = ring.tile([P, UNIT], U32, name="h_codes", align_bytes=64)
+            h_scales = ring.tile([P, UNIT], U8, name="h_scales", align_bytes=64)
+            nc.vector.quantize_mx(h_codes[:].bitcast(FP8X4), h_scales[:], h_grouped[:])
+            y_ps = psum.tile([P, UNIT], F32, name="y_ps", bufs=1)
+            nc.tensor.matmul_mx(
+                out=y_ps[:],
+                lhsT=w2_sb[:, e, :].bitcast(FP4X4),
+                lhsT_scale=w2_plane[:, e, :],
+                rhs=h_codes[:].bitcast(FP8X4),
+                rhs_scale=h_scales[:],
+                start=True,
+                stop=True,
+            )
+            nc.scalar.copy(y_sb[:, u * UNIT : (u + 1) * UNIT], y_ps[:])
+
+        for u0, units in GROUPS:
+            for s in range(PASSES):
+                first_layer(u0, units, s)
+            for u in range(u0, u0 + units):
+                second_layer(u)
+
+        for lo, n in OUT_PIECES:
+            one = ring.tile([P, n], F32, name=f"one_{lo}")
+            two = ring.tile([P, n], F32, name=f"two_{lo}")
+            both = ring.tile([P, n], F32, name=f"both_{lo}")
+            nc.vector.tensor_copy(one[:], y_sb[:].indirect(pos1_sb[:, lo // 16 : (lo + n) // 16]))
+            nc.vector.tensor_copy(two[:], y_sb[:].indirect(pos2_sb[:, lo // 16 : (lo + n) // 16]))
+            nc.vector.tensor_tensor(both[:], one[:], two[:], ADD)
+            nc.sync.dma_start(out[:, lo : lo + n], both[:])

@@ -9,7 +9,9 @@ P = 128
 PACK = 4
 PASSES = K // (P * PACK)
 UNIT = 128
-GROUPS = [(0, 4), (4, 3), (7, 2), (9, 1)]
+STEPS = [(0, 4, 0), (0, 4, 1), (0, 4, 2), (4, 3, 0), (4, 3, 1), (4, 3, 2), (7, 3, 0), (7, 2, 1), (7, 2, 2), (9, 1, 1), (9, 1, 2)]
+H_RUNS = [(0, 4), (4, 2), (6, 2), (8, 1), (9, 1)]
+GATE_CUTS = [0, 256, 512, S]
 OUT_PIECES = [(0, 384), (384, 256)]
 
 FLOPS = 2 * S * (K * H + H * N)
@@ -29,7 +31,12 @@ SILU = mybir.ActivationFunctionType.Silu
 
 
 def chunks(units):
-    return [(a, min(2, units - a)) for a in range(0, units, 2)]
+    runs, a = [], 0
+    while a < units:
+        m = max(w for w in (4, 2, 1) if w <= units - a)
+        runs.append((a, m))
+        a += m
+    return runs
 
 
 def tile_moe_pre_mlp_silu_kernel(
@@ -46,9 +53,7 @@ def tile_moe_pre_mlp_silu_kernel(
         pos2_sb = held.tile([P, T // 16], U16, name="pos2_sb")
         x_rows = xT.rearrange("(s p j) t -> s j p t", p=P, j=PACK)
         x_sb = {(s, j): held.tile([P, T], F32, name=f"x_{s}_{j}") for s in range(PASSES) for j in range(PACK)}
-        first = GROUPS[0][1] * UNIT
-        gate_a = held.tile([P, first], F32, name="gate_a")
-        gate_b = held.tile([P, S - first], F32, name="gate_b")
+        gate_sb = held.tile([P, S], F32, name="gate_sb")
         w1_sb = [held.tile([P, PASSES, 2 * H], U8, name=f"w1_{e}", align_bytes=64) for e in range(E)]
         w2_sb = held.tile([P, E, 2 * N], U8, name="w2_sb", align_bytes=64)
         w1_plane = held.tile([P, E * PASSES, H], U8, name="w1_plane", align_bytes=64)
@@ -60,9 +65,16 @@ def tile_moe_pre_mlp_silu_kernel(
         nc.vector.memset(w2_plane[:].rearrange("p a i -> p (a i)").bitcast(I32), 0)
         make_identity(nc, ident[:])
 
-        def load_x(s):
-            for j in range(PACK):
+        warm = held.tile([P, 1], F32, name="warm")
+        nc.scalar.activation(warm[:], ident[:, 0:1], SILU)
+
+        def load_x(s, planes):
+            for j in planes:
                 nc.sync.dma_start(x_sb[s, j][:], x_rows[s, j])
+
+        def load_gate(queue, c):
+            cols = slice(GATE_CUTS[c], GATE_CUTS[c + 1])
+            queue.dma_start(gate_sb[:, cols], gate[0:P, cols])
 
         def load_w1(e):
             nc.sync.dma_start(w1_sb[e][:].bitcast(I32), w1_words[e].rearrange("s p b -> p s b").bitcast(I32))
@@ -72,48 +84,63 @@ def tile_moe_pre_mlp_silu_kernel(
             for quad in range(4):
                 nc.sync.dma_start(plane[32 * quad : 32 * quad + 4, lo:hi, :].bitcast(I32), rows[4 * quad : 4 * quad + 4, lo:hi, :])
 
+        load_x(0, [0])
         nc.sync.dma_start(offs_sb[:], offs)
-        nc.sync.dma_start(gate_a[:], gate[0:P, 0:first])
-        load_x(0)
-        load_x(1)
+        load_gate(nc.scalar, 0)
+        load_gate(nc.sync, 1)
+        load_x(0, [1, 2, 3])
+        load_x(1, range(PACK))
         load_plane(w1_plane, w1_scales, 0, 2 * PASSES)
         load_w1(0)
-        load_x(2)
+        load_x(2, range(PACK))
         load_w1(1)
-        nc.sync.dma_start(gate_b[:], gate[0:P, first:S])
-        nc.sync.dma_start(w2_sb[:].bitcast(I32), w2_words.rearrange("e s p b -> p (e s) b").bitcast(I32))
+        load_gate(nc.sync, 2)
         load_plane(w1_plane, w1_scales, 2 * PASSES, E * PASSES)
         load_plane(w2_plane, w2_scales, 0, E)
         for e in range(2, E):
             load_w1(e)
+        nc.sync.dma_start(w2_sb[:].bitcast(I32), w2_words.rearrange("e s p b -> p (e s) b").bitcast(I32))
         nc.sync.dma_start(pos1_sb[:], pos1)
         nc.sync.dma_start(pos2_sb[:], pos2)
 
-        widest = max(units for u0, units in GROUPS) * UNIT
-        acc = {}
+        acc, picked, grouped = {}, {}, {}
+        h_grouped = held.tile([P, S * PACK], BF16, name="h_grouped", align_bytes=64)
+        h_codes = held.tile([P, S], U32, name="h_codes", align_bytes=64)
+        h_scales = held.tile([P, S], U8, name="h_scales", align_bytes=64)
 
-        def first_layer(u0, units, s):
-            lo, n = u0 * UNIT, units * UNIT
-            gate_sb = gate_a[:, lo : lo + n] if lo < first else gate_b[:, lo - first : lo - first + n]
-            picked = ring.tile([P, PACK, widest], F32, name="picked")
-            for j in range(PACK):
-                window = x_sb[s, j][:].indirect(offs_sb[:, lo // 16 : (lo + n) // 16])
-                nc.vector.tensor_tensor(picked[:, j, 0:n], window, gate_sb, MULT)
-            grouped = ring.tile([P, widest, PACK], BF16, name="grouped", align_bytes=64)
-            codes = ring.tile([P, widest], U32, name="codes", align_bytes=64)
-            scales = ring.tile([P, widest], U8, name="scales", align_bytes=64)
+        def gather(k, j):
+            u0, units, s = STEPS[k]
+            lo, hi = u0 * UNIT, (u0 + units) * UNIT
+            if j == 0:
+                picked[k] = ring.tile([P, PACK, hi - lo], F32, name=f"picked_{k}", tag="picked", bufs=2)
+            ends = GATE_CUTS[:3] if (k, j) == (0, 0) else [lo, hi]
+            for a, b in zip(ends, ends[1:]):
+                window = x_sb[s, j][:].indirect(offs_sb[:, a // 16 : b // 16])
+                nc.vector.tensor_tensor(picked[k][:, j, a - lo : b - lo], window, gate_sb[:, a:b], MULT)
+
+        def cast(k):
+            u0, units, s = STEPS[k]
+            grouped[k] = held.tile([P, units * UNIT, PACK], BF16, name=f"grouped_{k}", align_bytes=64)
             for a, m in chunks(units):
                 cols = slice(a * UNIT, (a + m) * UNIT)
-                nc.scalar.copy(
-                    grouped[:, cols, :].rearrange("p (c i) t -> p c t i", i=4),
-                    picked[:, :, cols].rearrange("p t (c i) -> p c t i", i=4),
+                copy = nc.vector.tensor_copy if k == len(STEPS) - 1 else nc.scalar.copy
+                copy(
+                    grouped[k][:, cols, :].rearrange("p (c i) t -> p c t i", i=4),
+                    picked[k][:, :, cols].rearrange("p t (c i) -> p c t i", i=4),
                 )
-                nc.vector.quantize_mx(codes[:, cols].bitcast(FP8X4), scales[:, cols], grouped[:, cols, :].rearrange("p c t -> p (c t)"))
+
+        def first_layer(k):
+            u0, units, s = STEPS[k]
+            codes = held.tile([P, units * UNIT], U32, name=f"codes_{k}", align_bytes=64)
+            scales = held.tile([P, units * UNIT], U8, name=f"scales_{k}", align_bytes=64)
+            for a, m in chunks(units):
+                cols = slice(a * UNIT, (a + m) * UNIT)
+                nc.vector.quantize_mx(codes[:, cols].bitcast(FP8X4), scales[:, cols], grouped[k][:, cols, :].rearrange("p c t -> p (c t)"))
                 for b in range(a, a + m):
                     u = u0 + b
                     e = u * UNIT // C
                     if s == 0:
-                        acc[u] = psum.tile([P, H], F32, name="acc", bufs=5)
+                        acc[u] = psum.tile([P, H], F32, name=f"acc_{u}", tag="bank", bufs=6)
                     one = slice(b * UNIT, (b + 1) * UNIT)
                     nc.tensor.matmul_mx(
                         out=acc[u][:],
@@ -125,41 +152,56 @@ def tile_moe_pre_mlp_silu_kernel(
                         stop=(s == PASSES - 1),
                     )
 
-        def second_layer(u):
-            e = u * UNIT // C
+        def turn_hidden(u):
             hidden = ring.tile([P, 2, P, 2], BF16, name="hidden")
             nc.scalar.activation(hidden[:], acc[u][:].rearrange("c (p v d) -> c v p d", v=2, d=2), SILU)
             pairs = hidden[:].rearrange("c v p d -> c (v p d)").bitcast(F32)
             turned = psum.tile([P, 2, UNIT], F32, name="turned", bufs=2)
             for v in range(2):
                 nc.tensor.transpose(turned[:, v, :], pairs[:, v * P : (v + 1) * P], ident[:])
-            h_grouped = ring.tile([P, UNIT * PACK], BF16, name="h_grouped", align_bytes=64)
-            nc.scalar.copy(h_grouped[:].bitcast(F32).rearrange("p (c v) -> p c v", v=2), turned[:].rearrange("p v c -> p c v"))
-            h_codes = ring.tile([P, UNIT], U32, name="h_codes", align_bytes=64)
-            h_scales = ring.tile([P, UNIT], U8, name="h_scales", align_bytes=64)
-            nc.vector.quantize_mx(h_codes[:].bitcast(FP8X4), h_scales[:], h_grouped[:])
-            y_ps = psum.tile([P, UNIT], F32, name="y_ps", bufs=1)
-            nc.tensor.matmul_mx(
-                out=y_ps[:],
-                lhsT=w2_sb[:, e, :].bitcast(FP4X4),
-                lhsT_scale=w2_plane[:, e, :],
-                rhs=h_codes[:].bitcast(FP8X4),
-                rhs_scale=h_scales[:],
-                start=True,
-                stop=True,
-            )
-            nc.scalar.copy(y_sb[:, u * UNIT : (u + 1) * UNIT], y_ps[:])
+            words = h_grouped[:, u * UNIT * PACK : (u + 1) * UNIT * PACK].bitcast(F32)
+            nc.scalar.copy(words.rearrange("p (c v) -> p c v", v=2), turned[:].rearrange("p v c -> p c v"))
 
-        for u0, units in GROUPS:
-            for s in range(PASSES):
-                first_layer(u0, units, s)
-            for u in range(u0, u0 + units):
-                second_layer(u)
+        def second_layer(u0, units):
+            lo, hi = u0 * UNIT, (u0 + units) * UNIT
+            nc.vector.quantize_mx(h_codes[:, lo:hi].bitcast(FP8X4), h_scales[:, lo:hi], h_grouped[:, lo * PACK : hi * PACK])
+            y_ps = psum.tile([P, hi - lo], F32, name=f"y_{u0}", tag="bank", bufs=6)
+            for a in range(lo, hi, C):
+                b = min(a + C, hi)
+                nc.tensor.matmul_mx(
+                    out=y_ps[:, a - lo : b - lo],
+                    lhsT=w2_sb[:, a // C, :].bitcast(FP4X4),
+                    lhsT_scale=w2_plane[:, a // C, :],
+                    rhs=h_codes[:, a:b].bitcast(FP8X4),
+                    rhs_scale=h_scales[:, a:b],
+                    start=True,
+                    stop=True,
+                )
+            if units > 1:
+                nc.vector.tensor_copy(y_sb[:, lo:hi], y_ps[:])
+            else:
+                nc.scalar.copy(y_sb[:, lo:hi], y_ps[:])
+
+        last = len(STEPS) - 1
+        for k in range(len(STEPS)):
+            for j in range(PACK):
+                gather(k, j)
+                if k > 0 and j == PACK - 1:
+                    first_layer(k - 1)
+            cast(k)
+            if k > 0 and k < last - 1 and STEPS[k - 1][2] == PASSES - 1:
+                for u in range(STEPS[k - 1][0], STEPS[k - 1][0] + STEPS[k - 1][1]):
+                    turn_hidden(u)
+        first_layer(last)
+        for u in range(STEPS[last - 2][0], S // UNIT):
+            turn_hidden(u)
+        for u0, units in H_RUNS:
+            second_layer(u0, units)
 
         for lo, n in OUT_PIECES:
-            one = ring.tile([P, n], F32, name=f"one_{lo}")
-            two = ring.tile([P, n], F32, name=f"two_{lo}")
-            both = ring.tile([P, n], F32, name=f"both_{lo}")
+            one = held.tile([P, n], F32, name=f"one_{lo}")
+            two = held.tile([P, n], F32, name=f"two_{lo}")
+            both = held.tile([P, n], F32, name=f"both_{lo}")
             nc.vector.tensor_copy(one[:], y_sb[:].indirect(pos1_sb[:, lo // 16 : (lo + n) // 16]))
             nc.vector.tensor_copy(two[:], y_sb[:].indirect(pos2_sb[:, lo // 16 : (lo + n) // 16]))
             nc.vector.tensor_tensor(both[:], one[:], two[:], ADD)

@@ -9,10 +9,12 @@ P = 128
 PACK = 4
 PASSES = K // (P * PACK)
 UNIT = 128
-STEPS = [(0, 4, 0), (0, 4, 1), (0, 4, 2), (4, 3, 0), (4, 3, 1), (4, 3, 2), (7, 3, 0), (7, 2, 1), (7, 2, 2), (9, 1, 1), (9, 1, 2)]
-H_RUNS = [(0, 4), (4, 2), (6, 2), (8, 1), (9, 1)]
+STEPS = [(u0, units, s) for u0, units in [(0, 4), (4, 3), (7, 2), (9, 1)] for s in range(PASSES)]
+Y_RUNS = [(0, 4, "scalar"), (4, 4, "vector"), (8, 1, "vector"), (9, 1, "vector")]
+TURNS = {3: [0, 1], 4: [2, 3], 6: [4, 5], 7: [6], 9: [7], 10: [8]}
+H_RUNS = [(0, 2), (2, 2), (4, 4), (8, 1), (9, 1)]
 GATE_CUTS = [0, 256, 512, S]
-OUT_PIECES = [(0, 384), (384, 256)]
+OUT_PIECES = [(0, 320), (320, 320)]
 
 FLOPS = 2 * S * (K * H + H * N)
 BYTES = 4 * K * T + E * (K * H + H * N) // 2 + E * (K * H + H * N) // 32 + 4 * S + 2 * P * (S + 2 * T) // 16 + 4 * N * T
@@ -103,10 +105,9 @@ def tile_moe_pre_mlp_silu_kernel(
         nc.sync.dma_start(pos1_sb[:], pos1)
         nc.sync.dma_start(pos2_sb[:], pos2)
 
-        acc, picked, grouped = {}, {}, {}
+        acc, picked, grouped, y_ps = {}, {}, {}, {}
         h_grouped = held.tile([P, S * PACK], BF16, name="h_grouped", align_bytes=64)
         h_codes = held.tile([P, S], U32, name="h_codes", align_bytes=64)
-        h_scales = held.tile([P, S], U8, name="h_scales", align_bytes=64)
 
         def gather(k, j):
             u0, units, s = STEPS[k]
@@ -120,7 +121,8 @@ def tile_moe_pre_mlp_silu_kernel(
 
         def cast(k):
             u0, units, s = STEPS[k]
-            grouped[k] = held.tile([P, units * UNIT, PACK], BF16, name=f"grouped_{k}", align_bytes=64)
+            tag = "late" if k == len(STEPS) - 1 else f"grouped_{k}"
+            grouped[k] = held.tile([P, units * UNIT, PACK], BF16, name=f"grouped_{k}", tag=tag, align_bytes=64)
             for a, m in chunks(units):
                 cols = slice(a * UNIT, (a + m) * UNIT)
                 copy = nc.vector.tensor_copy if k == len(STEPS) - 1 else nc.scalar.copy
@@ -154,7 +156,8 @@ def tile_moe_pre_mlp_silu_kernel(
 
         def turn_hidden(u):
             hidden = ring.tile([P, 2, P, 2], BF16, name="hidden")
-            nc.scalar.activation(hidden[:], acc[u][:].rearrange("c (p v d) -> c v p d", v=2, d=2), SILU)
+            sums = acc[u][:].rearrange("c (p v d) -> c v p d", v=2, d=2)
+            nc.scalar.activation(hidden[:], sums, SILU)
             pairs = hidden[:].rearrange("c v p d -> c (v p d)").bitcast(F32)
             turned = psum.tile([P, 2, UNIT], F32, name="turned", bufs=2)
             for v in range(2):
@@ -162,14 +165,17 @@ def tile_moe_pre_mlp_silu_kernel(
             words = h_grouped[:, u * UNIT * PACK : (u + 1) * UNIT * PACK].bitcast(F32)
             nc.scalar.copy(words.rearrange("p (c v) -> p c v", v=2), turned[:].rearrange("p v c -> p c v"))
 
-        def second_layer(u0, units):
+        def second_layer(u0, units, h_scales):
             lo, hi = u0 * UNIT, (u0 + units) * UNIT
             nc.vector.quantize_mx(h_codes[:, lo:hi].bitcast(FP8X4), h_scales[:, lo:hi], h_grouped[:, lo * PACK : hi * PACK])
-            y_ps = psum.tile([P, hi - lo], F32, name=f"y_{u0}", tag="bank", bufs=6)
+            first, count, engine = [run for run in Y_RUNS if run[0] <= u0][-1]
+            if u0 == first:
+                y_ps[first] = psum.tile([P, count * UNIT], F32, name=f"y_{u0}", tag="bank", bufs=6)
+            base = first * UNIT
             for a in range(lo, hi, C):
                 b = min(a + C, hi)
                 nc.tensor.matmul_mx(
-                    out=y_ps[:, a - lo : b - lo],
+                    out=y_ps[first][:, a - base : b - base],
                     lhsT=w2_sb[:, a // C, :].bitcast(FP4X4),
                     lhsT_scale=w2_plane[:, a // C, :],
                     rhs=h_codes[:, a:b].bitcast(FP8X4),
@@ -177,10 +183,9 @@ def tile_moe_pre_mlp_silu_kernel(
                     start=True,
                     stop=True,
                 )
-            if units > 1:
-                nc.vector.tensor_copy(y_sb[:, lo:hi], y_ps[:])
-            else:
-                nc.scalar.copy(y_sb[:, lo:hi], y_ps[:])
+            if u0 + units == first + count:
+                copy = nc.scalar.copy if engine == "scalar" else nc.vector.tensor_copy
+                copy(y_sb[:, base:hi], y_ps[first][:])
 
         last = len(STEPS) - 1
         for k in range(len(STEPS)):
@@ -189,20 +194,24 @@ def tile_moe_pre_mlp_silu_kernel(
                 if k > 0 and j == PACK - 1:
                     first_layer(k - 1)
             cast(k)
-            if k > 0 and k < last - 1 and STEPS[k - 1][2] == PASSES - 1:
-                for u in range(STEPS[k - 1][0], STEPS[k - 1][0] + STEPS[k - 1][1]):
-                    turn_hidden(u)
+            for u in TURNS.get(k, []):
+                turn_hidden(u)
         first_layer(last)
-        for u in range(STEPS[last - 2][0], S // UNIT):
+        for u in range(STEPS[last][0], S // UNIT):
             turn_hidden(u)
+        early_scales = held.tile([P, S], U8, name="early_scales", align_bytes=64)
+        late_scales = held.tile([P, S], U8, name="late_scales", tag="late", align_bytes=64)
         for u0, units in H_RUNS:
-            second_layer(u0, units)
+            second_layer(u0, units, early_scales if u0 < 1 else late_scales)
 
+        fetched = []
         for lo, n in OUT_PIECES:
             one = held.tile([P, n], F32, name=f"one_{lo}")
             two = held.tile([P, n], F32, name=f"two_{lo}")
-            both = held.tile([P, n], F32, name=f"both_{lo}")
             nc.vector.tensor_copy(one[:], y_sb[:].indirect(pos1_sb[:, lo // 16 : (lo + n) // 16]))
             nc.vector.tensor_copy(two[:], y_sb[:].indirect(pos2_sb[:, lo // 16 : (lo + n) // 16]))
+            fetched.append((lo, n, one, two))
+        for lo, n, one, two in fetched:
+            both = held.tile([P, n], F32, name=f"both_{lo}")
             nc.vector.tensor_tensor(both[:], one[:], two[:], ADD)
             nc.sync.dma_start(out[:, lo : lo + n], both[:])

@@ -11,7 +11,7 @@ PASSES = K // (P * PACK)
 UNIT = 128
 STEPS = [(u0, units, s) for u0, units in [(0, 4), (4, 3), (7, 2), (9, 1)] for s in range(PASSES)]
 Y_RUNS = [(0, 4, "scalar"), (4, 4, "vector"), (8, 1, "vector"), (9, 1, "vector")]
-TURNS = {3: [0, 1], 4: [2, 3], 6: [4, 5], 7: [6], 9: [7], 10: [8]}
+TURNS = {3: [0, 1], 4: [2, 3], 6: [4, 5], 8: [6], 9: [7], 10: [8]}
 H_RUNS = [(0, 2), (2, 2), (4, 4), (8, 1), (9, 1)]
 GATE_CUTS = [0, 256, 512, S]
 OUT_PIECES = [(0, 320), (320, 320)]
@@ -66,9 +66,6 @@ def tile_moe_pre_mlp_silu_kernel(
         nc.vector.memset(w1_plane[:].rearrange("p a i -> p (a i)").bitcast(I32), 0)
         nc.vector.memset(w2_plane[:].rearrange("p a i -> p (a i)").bitcast(I32), 0)
         make_identity(nc, ident[:])
-
-        warm = held.tile([P, 1], F32, name="warm")
-        nc.scalar.activation(warm[:], ident[:, 0:1], SILU)
 
         def load_x(s, planes):
             for j in planes:

@@ -9,12 +9,18 @@ P = 128
 PACK = 4
 PASSES = K // (P * PACK)
 UNIT = 128
-STEPS = [(u0, units, s) for u0, units in [(0, 4), (4, 3), (7, 2), (9, 1)] for s in range(PASSES)]
-Y_RUNS = [(0, 4, "scalar"), (4, 4, "vector"), (8, 1, "vector"), (9, 1, "vector")]
-TURNS = {3: [0, 1], 4: [2, 3], 6: [4, 5], 8: [6], 9: [7], 10: [8]}
+SPARE = 16
+STEPS = [(0, 5, 0), (0, 5, 1), (0, 8, 2), (5, 3, 0), (5, 5, 1), (8, 2, 0), (8, 1, 2), (9, 1, 2)]
+Y_RUNS = [(0, 4, "vector"), (4, 4, "vector"), (8, 1, "vector"), (9, 1, "vector")]
+TURNS = {3: [0, 1, 2, 3, 4], 5: [5], 6: [6, 7], 7: [8], 8: [9]}
 H_RUNS = [(0, 2), (2, 2), (4, 4), (8, 1), (9, 1)]
-GATE_CUTS = [0, 256, 512, S]
-OUT_PIECES = [(0, 320), (320, 320)]
+HELD_BACK = {(2, 5), (2, 6), (2, 7)}
+ACC_BANK = [0, 1, 2, 3, 4, 4, 5, 6, 0, 1]
+TURN_BANK = [5, 6, 7, 5, 6, 7, 2, 3, 7, 2]
+Y_BANK = {0: 4, 4: 5, 8: 6, 9: 3}
+CAST_BEHIND = {4: "hidden_3", 5: "hidden_4"}
+GATE_CUTS = [0, 256, 640, 1024, S]
+OUT_PIECES = [(0, 384), (384, 256)]
 
 FLOPS = 2 * S * (K * H + H * N)
 BYTES = 4 * K * T + E * (K * H + H * N) // 2 + E * (K * H + H * N) // 32 + 4 * S + 2 * P * (S + 2 * T) // 16 + 4 * N * T
@@ -50,11 +56,14 @@ def tile_moe_pre_mlp_silu_kernel(
         ring = ctx.enter_context(tc.tile_pool(name="ring", bufs=3))
         psum = ctx.enter_context(tc.psum_pool(name="psum", bufs=1))
 
+        last = len(STEPS) - 1
         offs_sb = held.tile([P, S // 16], U16, name="offs_sb")
         pos1_sb = held.tile([P, T // 16], U16, name="pos1_sb")
         pos2_sb = held.tile([P, T // 16], U16, name="pos2_sb")
         x_rows = xT.rearrange("(s p j) t -> s j p t", p=P, j=PACK)
-        x_sb = {(s, j): held.tile([P, T], F32, name=f"x_{s}_{j}") for s in range(PASSES) for j in range(PACK)}
+        widest = [max(units * UNIT for u0, units, s in STEPS if s == a) for a in range(PASSES)]
+        width = [T if widest[s] < T else widest[s] + SPARE for s in range(PASSES)]
+        x_sb = {(s, j): held.tile([P, width[s]], F32, name=f"x_{s}_{j}", align_bytes=64) for s in range(PASSES) for j in range(PACK)}
         gate_sb = held.tile([P, S], F32, name="gate_sb")
         w1_sb = [held.tile([P, PASSES, 2 * H], U8, name=f"w1_{e}", align_bytes=64) for e in range(E)]
         w2_sb = held.tile([P, E, 2 * N], U8, name="w2_sb", align_bytes=64)
@@ -65,11 +74,15 @@ def tile_moe_pre_mlp_silu_kernel(
 
         nc.vector.memset(w1_plane[:].rearrange("p a i -> p (a i)").bitcast(I32), 0)
         nc.vector.memset(w2_plane[:].rearrange("p a i -> p (a i)").bitcast(I32), 0)
+        for s in range(PASSES):
+            for j in range(PACK):
+                if width[s] > T:
+                    nc.gpsimd.memset(x_sb[s, j][:, T:], 0.0)
         make_identity(nc, ident[:])
 
         def load_x(s, planes):
             for j in planes:
-                nc.sync.dma_start(x_sb[s, j][:], x_rows[s, j])
+                nc.sync.dma_start(x_sb[s, j][:, 0:T], x_rows[s, j])
 
         def load_gate(queue, c):
             cols = slice(GATE_CUTS[c], GATE_CUTS[c + 1])
@@ -89,20 +102,18 @@ def tile_moe_pre_mlp_silu_kernel(
         load_gate(nc.sync, 1)
         load_x(0, [1, 2, 3])
         load_x(1, range(PACK))
-        load_plane(w1_plane, w1_scales, 0, 2 * PASSES)
-        load_w1(0)
-        load_x(2, range(PACK))
-        load_w1(1)
         load_gate(nc.sync, 2)
-        load_plane(w1_plane, w1_scales, 2 * PASSES, E * PASSES)
+        load_x(2, range(PACK))
+        load_gate(nc.sync, 3)
+        load_plane(w1_plane, w1_scales, 0, E * PASSES)
         load_plane(w2_plane, w2_scales, 0, E)
-        for e in range(2, E):
+        for e in range(E):
             load_w1(e)
         nc.sync.dma_start(w2_sb[:].bitcast(I32), w2_words.rearrange("e s p b -> p (e s) b").bitcast(I32))
         nc.sync.dma_start(pos1_sb[:], pos1)
         nc.sync.dma_start(pos2_sb[:], pos2)
 
-        acc, picked, grouped, y_ps = {}, {}, {}, {}
+        acc, picked, grouped, y_ps, waiting, done = {}, {}, {}, {}, {}, {}
         h_grouped = held.tile([P, S * PACK], BF16, name="h_grouped", align_bytes=64)
         h_codes = held.tile([P, S], U32, name="h_codes", align_bytes=64)
 
@@ -118,11 +129,10 @@ def tile_moe_pre_mlp_silu_kernel(
 
         def cast(k):
             u0, units, s = STEPS[k]
-            tag = "late" if k == len(STEPS) - 1 else f"grouped_{k}"
-            grouped[k] = held.tile([P, units * UNIT, PACK], BF16, name=f"grouped_{k}", tag=tag, align_bytes=64)
+            grouped[k] = held.tile([P, units * UNIT, PACK], BF16, name=f"grouped_{k}", tag=CAST_BEHIND.get(k, f"grouped_{k}"), align_bytes=64)
             for a, m in chunks(units):
                 cols = slice(a * UNIT, (a + m) * UNIT)
-                copy = nc.vector.tensor_copy if k == len(STEPS) - 1 else nc.scalar.copy
+                copy = nc.vector.tensor_copy if k == last else nc.scalar.copy
                 copy(
                     grouped[k][:, cols, :].rearrange("p (c i) t -> p c t i", i=4),
                     picked[k][:, :, cols].rearrange("p t (c i) -> p c t i", i=4),
@@ -138,25 +148,31 @@ def tile_moe_pre_mlp_silu_kernel(
                 for b in range(a, a + m):
                     u = u0 + b
                     e = u * UNIT // C
-                    if s == 0:
-                        acc[u] = psum.tile([P, H], F32, name=f"acc_{u}", tag="bank", bufs=6)
                     one = slice(b * UNIT, (b + 1) * UNIT)
-                    nc.tensor.matmul_mx(
-                        out=acc[u][:],
-                        lhsT=codes[:, one].bitcast(FP8X4),
-                        lhsT_scale=scales[:, one],
-                        rhs=w1_sb[e][:, s, :].bitcast(FP4X4),
-                        rhs_scale=w1_plane[:, e * PASSES + s, :],
-                        start=(s == 0),
-                        stop=(s == PASSES - 1),
-                    )
+                    waiting.setdefault(u, []).append((s, codes[:, one], scales[:, one]))
+                    if (k, u) in HELD_BACK:
+                        continue
+                    for s1, words, plane in waiting.pop(u):
+                        n = done.get(u, 0)
+                        if n == 0:
+                            acc[u] = psum.tile([P, H], F32, name=f"acc_{u}", tag=f"bank_{ACC_BANK[u]}")
+                        nc.tensor.matmul_mx(
+                            out=acc[u][:],
+                            lhsT=words.bitcast(FP8X4),
+                            lhsT_scale=plane,
+                            rhs=w1_sb[e][:, s1, :].bitcast(FP4X4),
+                            rhs_scale=w1_plane[:, e * PASSES + s1, :],
+                            start=(n == 0),
+                            stop=(n == PASSES - 1),
+                        )
+                        done[u] = n + 1
 
         def turn_hidden(u):
-            hidden = ring.tile([P, 2, P, 2], BF16, name="hidden")
+            hidden = held.tile([P, 2, P, 2], BF16, name=f"hidden_{u}", align_bytes=64)
             sums = acc[u][:].rearrange("c (p v d) -> c v p d", v=2, d=2)
             nc.scalar.activation(hidden[:], sums, SILU)
             pairs = hidden[:].rearrange("c v p d -> c (v p d)").bitcast(F32)
-            turned = psum.tile([P, 2, UNIT], F32, name="turned", bufs=2)
+            turned = psum.tile([P, 2, UNIT], F32, name=f"turned_{u}", tag=f"bank_{TURN_BANK[u]}")
             for v in range(2):
                 nc.tensor.transpose(turned[:, v, :], pairs[:, v * P : (v + 1) * P], ident[:])
             words = h_grouped[:, u * UNIT * PACK : (u + 1) * UNIT * PACK].bitcast(F32)
@@ -167,10 +183,10 @@ def tile_moe_pre_mlp_silu_kernel(
             nc.vector.quantize_mx(h_codes[:, lo:hi].bitcast(FP8X4), h_scales[:, lo:hi], h_grouped[:, lo * PACK : hi * PACK])
             first, count, engine = [run for run in Y_RUNS if run[0] <= u0][-1]
             if u0 == first:
-                y_ps[first] = psum.tile([P, count * UNIT], F32, name=f"y_{u0}", tag="bank", bufs=6)
+                y_ps[first] = psum.tile([P, count * UNIT], F32, name=f"y_{u0}", tag=f"bank_{Y_BANK[first]}")
             base = first * UNIT
-            for a in range(lo, hi, C):
-                b = min(a + C, hi)
+            cuts = sorted({lo, hi} | {a for a in range(0, S, C) if lo < a < hi})
+            for a, b in zip(cuts, cuts[1:]):
                 nc.tensor.matmul_mx(
                     out=y_ps[first][:, a - base : b - base],
                     lhsT=w2_sb[:, a // C, :].bitcast(FP4X4),
@@ -184,7 +200,6 @@ def tile_moe_pre_mlp_silu_kernel(
                 copy = nc.scalar.copy if engine == "scalar" else nc.vector.tensor_copy
                 copy(y_sb[:, base:hi], y_ps[first][:])
 
-        last = len(STEPS) - 1
         for k in range(len(STEPS)):
             for j in range(PACK):
                 gather(k, j)
@@ -194,21 +209,18 @@ def tile_moe_pre_mlp_silu_kernel(
             for u in TURNS.get(k, []):
                 turn_hidden(u)
         first_layer(last)
-        for u in range(STEPS[last][0], S // UNIT):
+        for u in TURNS[last + 1]:
             turn_hidden(u)
-        early_scales = held.tile([P, S], U8, name="early_scales", align_bytes=64)
-        late_scales = held.tile([P, S], U8, name="late_scales", tag="late", align_bytes=64)
+        late_scales = held.tile([P, S], U8, name="late_scales", tag=f"x_{STEPS[last][2]}_{PACK - 1}", align_bytes=64)
         for u0, units in H_RUNS:
-            second_layer(u0, units, early_scales if u0 < 1 else late_scales)
+            second_layer(u0, units, late_scales)
 
         fetched = []
         for lo, n in OUT_PIECES:
             one = held.tile([P, n], F32, name=f"one_{lo}")
-            two = held.tile([P, n], F32, name=f"two_{lo}")
             nc.vector.tensor_copy(one[:], y_sb[:].indirect(pos1_sb[:, lo // 16 : (lo + n) // 16]))
-            nc.vector.tensor_copy(two[:], y_sb[:].indirect(pos2_sb[:, lo // 16 : (lo + n) // 16]))
-            fetched.append((lo, n, one, two))
-        for lo, n, one, two in fetched:
+            fetched.append((lo, n, one))
+        for lo, n, one in fetched:
             both = held.tile([P, n], F32, name=f"both_{lo}")
-            nc.vector.tensor_tensor(both[:], one[:], two[:], ADD)
+            nc.vector.tensor_tensor(both[:], y_sb[:].indirect(pos2_sb[:, lo // 16 : (lo + n) // 16]), one[:], ADD)
             nc.sync.dma_start(out[:, lo : lo + n], both[:])

@@ -11,16 +11,17 @@ PASSES = K // (P * PACK)
 UNIT = 128
 SPARE = 16
 STEPS = [(0, 5, 0), (0, 5, 1), (0, 8, 2), (5, 3, 0), (5, 5, 1), (8, 2, 0), (8, 1, 2), (9, 1, 2)]
-Y_RUNS = [(0, 4, "vector"), (4, 4, "vector"), (8, 1, "vector"), (9, 1, "vector")]
-TURNS = {3: [0, 1, 2, 3, 4], 5: [5], 6: [6, 7], 7: [8], 8: [9]}
-H_RUNS = [(0, 2), (2, 2), (4, 4), (8, 1), (9, 1)]
+Y_RUNS = [(0, 4, "vector"), (4, 4, "scalar"), (8, 1, "scalar"), (9, 1, "vector")]
 HELD_BACK = {(2, 5), (2, 6), (2, 7)}
 ACC_BANK = [0, 1, 2, 3, 4, 4, 5, 6, 0, 1]
-TURN_BANK = [5, 6, 7, 5, 6, 7, 2, 3, 7, 2]
-Y_BANK = {0: 4, 4: 5, 8: 6, 9: 3}
-CAST_BEHIND = {4: "hidden_3", 5: "hidden_4"}
-GATE_CUTS = [0, 256, 640, 1024, S]
-OUT_PIECES = [(0, 384), (384, 256)]
+TURN_BANK = [5, 6, 7, 5, 6, 7, 2, 3, 4, 5]
+Y_BANK = {0: 6, 4: 2, 8: 0, 9: 1}
+CAST_BEHIND = {4: "hidden_3", 5: "hidden_4", 6: "hidden_5"}
+H_TILES = [(0, 5, "h_grouped_0"), (5, 3, "grouped_7"), (8, 2, "h_grouped_8")]
+CODE_TILES = {6: (6, 2, "hidden_7"), 7: (6, 2, "hidden_7")}
+LATE_REST = {2, 4}
+GATE_CUTS = [0, 128, 640, 1024, S]
+OUT_PIECES = [(0, 448), (448, 192)]
 
 FLOPS = 2 * S * (K * H + H * N)
 BYTES = 4 * K * T + E * (K * H + H * N) // 2 + E * (K * H + H * N) // 32 + 4 * S + 2 * P * (S + 2 * T) // 16 + 4 * N * T
@@ -75,10 +76,11 @@ def tile_moe_pre_mlp_silu_kernel(
         nc.vector.memset(w1_plane[:].rearrange("p a i -> p (a i)").bitcast(I32), 0)
         nc.vector.memset(w2_plane[:].rearrange("p a i -> p (a i)").bitcast(I32), 0)
         for s in range(PASSES):
+            if s == 1:
+                make_identity(nc, ident[:])
             for j in range(PACK):
                 if width[s] > T:
                     nc.gpsimd.memset(x_sb[s, j][:, T:], 0.0)
-        make_identity(nc, ident[:])
 
         def load_x(s, planes):
             for j in planes:
@@ -114,7 +116,7 @@ def tile_moe_pre_mlp_silu_kernel(
         nc.sync.dma_start(pos2_sb[:], pos2)
 
         acc, picked, grouped, y_ps, waiting, done = {}, {}, {}, {}, {}, {}
-        h_grouped = held.tile([P, S * PACK], BF16, name="h_grouped", align_bytes=64)
+        hidden, turned, h_grouped, coded, scaled = {}, {}, {}, {}, {}
         h_codes = held.tile([P, S], U32, name="h_codes", align_bytes=64)
 
         def gather(k, j):
@@ -138,11 +140,17 @@ def tile_moe_pre_mlp_silu_kernel(
                     picked[k][:, :, cols].rearrange("p t (c i) -> p c t i", i=4),
                 )
 
-        def first_layer(k):
+        def first_layer(k, parts):
             u0, units, s = STEPS[k]
-            codes = held.tile([P, units * UNIT], U32, name=f"codes_{k}", align_bytes=64)
-            scales = held.tile([P, units * UNIT], U8, name=f"scales_{k}", align_bytes=64)
-            for a, m in chunks(units):
+            first, count, tag = CODE_TILES.get(k, (k, units, f"codes_{k}"))
+            if first not in coded:
+                coded[first] = held.tile([P, count * UNIT], U32, name=f"codes_{first}", tag=tag, align_bytes=64)
+            skip = (u0 - STEPS[first][0]) * UNIT
+            codes = coded[first][:, skip : skip + units * UNIT]
+            if k not in scaled:
+                scaled[k] = held.tile([P, units * UNIT], U8, name=f"scales_{k}", align_bytes=64)
+            scales = scaled[k]
+            for a, m in chunks(units)[parts]:
                 cols = slice(a * UNIT, (a + m) * UNIT)
                 nc.vector.quantize_mx(codes[:, cols].bitcast(FP8X4), scales[:, cols], grouped[k][:, cols, :].rearrange("p c t -> p (c t)"))
                 for b in range(a, a + m):
@@ -167,20 +175,33 @@ def tile_moe_pre_mlp_silu_kernel(
                         )
                         done[u] = n + 1
 
-        def turn_hidden(u):
-            hidden = held.tile([P, 2, P, 2], BF16, name=f"hidden_{u}", align_bytes=64)
+        def silu(u):
+            hidden[u] = held.tile([P, 2, P, 2], BF16, name=f"hidden_{u}", align_bytes=64)
             sums = acc[u][:].rearrange("c (p v d) -> c v p d", v=2, d=2)
-            nc.scalar.activation(hidden[:], sums, SILU)
-            pairs = hidden[:].rearrange("c v p d -> c (v p d)").bitcast(F32)
-            turned = psum.tile([P, 2, UNIT], F32, name=f"turned_{u}", tag=f"bank_{TURN_BANK[u]}")
+            halves = [slice(0, 1), slice(1, 2)] if u == S // UNIT - 1 else [slice(0, 2)]
+            for half in halves:
+                nc.scalar.activation(hidden[u][:, half], sums[:, half], SILU)
+
+        def turn(u):
+            pairs = hidden[u][:].rearrange("c v p d -> c (v p d)").bitcast(F32)
+            turned[u] = psum.tile([P, 2, UNIT], F32, name=f"turned_{u}", tag=f"bank_{TURN_BANK[u]}")
             for v in range(2):
-                nc.tensor.transpose(turned[:, v, :], pairs[:, v * P : (v + 1) * P], ident[:])
-            words = h_grouped[:, u * UNIT * PACK : (u + 1) * UNIT * PACK].bitcast(F32)
-            nc.scalar.copy(words.rearrange("p (c v) -> p c v", v=2), turned[:].rearrange("p v c -> p c v"))
+                nc.tensor.transpose(turned[u][:, v, :], pairs[:, v * P : (v + 1) * P], ident[:])
+
+        def weave(u, engine):
+            words = h_rows(u, 1).bitcast(F32)
+            copy = nc.scalar.copy if engine == "scalar" else nc.vector.tensor_copy
+            copy(words.rearrange("p (c v) -> p c v", v=2), turned[u][:].rearrange("p v c -> p c v"))
+
+        def h_rows(u, units):
+            first, count, tag = [run for run in H_TILES if run[0] <= u][-1]
+            if first not in h_grouped:
+                h_grouped[first] = held.tile([P, count * UNIT * PACK], BF16, name=f"h_grouped_{first}", tag=tag, align_bytes=64)
+            return h_grouped[first][:, (u - first) * UNIT * PACK : (u - first + units) * UNIT * PACK]
 
         def second_layer(u0, units, h_scales):
             lo, hi = u0 * UNIT, (u0 + units) * UNIT
-            nc.vector.quantize_mx(h_codes[:, lo:hi].bitcast(FP8X4), h_scales[:, lo:hi], h_grouped[:, lo * PACK : hi * PACK])
+            nc.vector.quantize_mx(h_codes[:, lo:hi].bitcast(FP8X4), h_scales[:, lo:hi], h_rows(u0, units))
             first, count, engine = [run for run in Y_RUNS if run[0] <= u0][-1]
             if u0 == first:
                 y_ps[first] = psum.tile([P, count * UNIT], F32, name=f"y_{u0}", tag=f"bank_{Y_BANK[first]}")
@@ -196,24 +217,58 @@ def tile_moe_pre_mlp_silu_kernel(
                     start=True,
                     stop=True,
                 )
-            if u0 + units == first + count:
-                copy = nc.scalar.copy if engine == "scalar" else nc.vector.tensor_copy
-                copy(y_sb[:, base:hi], y_ps[first][:])
 
-        for k in range(len(STEPS)):
+        def fetch_sums(first, count, engine):
+            copy = nc.scalar.copy if engine == "scalar" else nc.vector.tensor_copy
+            copy(y_sb[:, first * UNIT : (first + count) * UNIT], y_ps[first][:])
+
+        def step(k):
             for j in range(PACK):
                 gather(k, j)
-                if k > 0 and j == PACK - 1:
-                    first_layer(k - 1)
+                if j == 0 and k - 2 in LATE_REST:
+                    first_layer(k - 2, slice(1, None))
+
+        def behind(k):
+            first_layer(k - 1, slice(0, 1) if k - 1 in LATE_REST else slice(None))
+
+        step(0)
+        cast(0)
+        for k in range(1, 4):
+            step(k)
+            behind(k)
             cast(k)
-            for u in TURNS.get(k, []):
-                turn_hidden(u)
-        first_layer(last)
-        for u in TURNS[last + 1]:
-            turn_hidden(u)
-        late_scales = held.tile([P, S], U8, name="late_scales", tag=f"x_{STEPS[last][2]}_{PACK - 1}", align_bytes=64)
-        for u0, units in H_RUNS:
+        step(4)
+        for u in range(5):
+            silu(u)
+            turn(u)
+            weave(u, "scalar")
+        behind(4)
+        cast(4)
+        step(5)
+        behind(5)
+        cast(5)
+        for u in (5, 6, 7):
+            silu(u)
+            turn(u)
+        for k in (6, 7):
+            step(k)
+            behind(k)
+            cast(k)
+        first_layer(last, slice(None))
+        for u in (8, 9):
+            silu(u)
+        for u in (8, 9):
+            turn(u)
+            weave(u, "scalar")
+        early_scales = held.tile([P, S], U8, name="early_scales", tag=f"x_{STEPS[last][2]}_{PACK - 1}", align_bytes=64)
+        late_scales = held.tile([P, S], U8, name="late_scales", tag=f"scales_{last}", align_bytes=64)
+        second_layer(0, 2, early_scales)
+        for u in (5, 6, 7):
+            weave(u, "vector")
+        for u0, units in [(2, 2), (4, 1), (5, 1), (6, 2), (8, 1), (9, 1)]:
             second_layer(u0, units, late_scales)
+        for run in Y_RUNS:
+            fetch_sums(*run)
 
         fetched = []
         for lo, n in OUT_PIECES:

@@ -11,13 +11,13 @@ PASSES = K // (P * PACK)
 UNIT = 128
 SPARE = 16
 STEPS = [(0, 5, 0), (0, 5, 1), (0, 8, 2), (5, 3, 0), (5, 5, 1), (8, 2, 0), (8, 1, 2), (9, 1, 2)]
-Y_RUNS = [(0, 4, "vector"), (4, 4, "scalar"), (8, 1, "scalar"), (9, 1, "vector")]
+Y_RUNS = [(0, 4, "scalar"), (4, 4, "vector"), (8, 1, "scalar"), (9, 1, "scalar")]
 HELD_BACK = {(2, 5), (2, 6), (2, 7)}
-ACC_BANK = [0, 1, 2, 3, 4, 4, 5, 6, 0, 1]
-TURN_BANK = [5, 6, 7, 5, 6, 7, 2, 3, 4, 5]
-Y_BANK = {0: 6, 4: 2, 8: 0, 9: 1}
+ACC_BANK = [0, 1, 2, 3, 4, 4, 6, 3, 0, 1]
+TURN_RUNS = [(0, 2, 5), (2, 2, 6), (4, 2, 7), (6, 2, 5), (8, 1, 2), (9, 1, 4)]
+Y_BANK = {0: 6, 4: 3, 8: 0, 9: 1}
 CAST_BEHIND = {4: "hidden_3", 5: "hidden_4", 6: "hidden_5"}
-H_TILES = [(0, 5, "h_grouped_0"), (5, 3, "grouped_7"), (8, 2, "h_grouped_8")]
+H_TILES = [(0, 4, "h_grouped_0"), (4, 4, "grouped_7"), (8, 2, "h_grouped_8")]
 CODE_TILES = {6: (6, 2, "hidden_7"), 7: (6, 2, "hidden_7")}
 LATE_REST = {2, 4}
 GATE_CUTS = [0, 128, 640, 1024, S]
@@ -134,8 +134,7 @@ def tile_moe_pre_mlp_silu_kernel(
             grouped[k] = held.tile([P, units * UNIT, PACK], BF16, name=f"grouped_{k}", tag=CAST_BEHIND.get(k, f"grouped_{k}"), align_bytes=64)
             for a, m in chunks(units):
                 cols = slice(a * UNIT, (a + m) * UNIT)
-                copy = nc.vector.tensor_copy if k == last else nc.scalar.copy
-                copy(
+                nc.scalar.copy(
                     grouped[k][:, cols, :].rearrange("p (c i) t -> p c t i", i=4),
                     picked[k][:, :, cols].rearrange("p t (c i) -> p c t i", i=4),
                 )
@@ -184,14 +183,16 @@ def tile_moe_pre_mlp_silu_kernel(
 
         def turn(u):
             pairs = hidden[u][:].rearrange("c v p d -> c (v p d)").bitcast(F32)
-            turned[u] = psum.tile([P, 2, UNIT], F32, name=f"turned_{u}", tag=f"bank_{TURN_BANK[u]}")
+            first, count, bank = [run for run in TURN_RUNS if run[0] <= u][-1]
+            if u == first:
+                turned[first] = psum.tile([P, count, 2, UNIT], F32, name=f"turned_{u}", tag=f"bank_{bank}")
             for v in range(2):
-                nc.tensor.transpose(turned[u][:, v, :], pairs[:, v * P : (v + 1) * P], ident[:])
+                nc.tensor.transpose(turned[first][:, u - first, v, :], pairs[:, v * P : (v + 1) * P], ident[:])
 
-        def weave(u, engine):
-            words = h_rows(u, 1).bitcast(F32)
+        def weave(first, count, engine):
+            words = h_rows(first, count).bitcast(F32)
             copy = nc.scalar.copy if engine == "scalar" else nc.vector.tensor_copy
-            copy(words.rearrange("p (c v) -> p c v", v=2), turned[u][:].rearrange("p v c -> p c v"))
+            copy(words.rearrange("p (u c v) -> p u c v", u=count, v=2), turned[first][:].rearrange("p u v c -> p u c v"))
 
         def h_rows(u, units):
             first, count, tag = [run for run in H_TILES if run[0] <= u][-1]
@@ -241,7 +242,8 @@ def tile_moe_pre_mlp_silu_kernel(
         for u in range(5):
             silu(u)
             turn(u)
-            weave(u, "scalar")
+            if u in (1, 3):
+                weave(u - 1, 2, "scalar")
         behind(4)
         cast(4)
         step(5)
@@ -259,13 +261,13 @@ def tile_moe_pre_mlp_silu_kernel(
             silu(u)
         for u in (8, 9):
             turn(u)
-            weave(u, "scalar")
+            weave(u, 1, "scalar")
         early_scales = held.tile([P, S], U8, name="early_scales", tag=f"x_{STEPS[last][2]}_{PACK - 1}", align_bytes=64)
         late_scales = held.tile([P, S], U8, name="late_scales", tag=f"scales_{last}", align_bytes=64)
         second_layer(0, 2, early_scales)
-        for u in (5, 6, 7):
-            weave(u, "vector")
-        for u0, units in [(2, 2), (4, 1), (5, 1), (6, 2), (8, 1), (9, 1)]:
+        for u in (4, 6):
+            weave(u, 2, "vector")
+        for u0, units in [(2, 2), (4, 4), (8, 1), (9, 1)]:
             second_layer(u0, units, late_scales)
         for run in Y_RUNS:
             fetch_sums(*run)

@@ -10,6 +10,7 @@ PACK = 4
 PASSES = K // (P * PACK)
 UNIT = 128
 SPARE = 16
+HALVED = (7, 9)
 STEPS = [(0, 5, 0), (0, 5, 1), (0, 8, 2), (5, 3, 0), (5, 5, 1), (8, 2, 0), (8, 1, 2), (9, 1, 2)]
 Y_RUNS = [(0, 4, "scalar"), (4, 4, "vector"), (8, 1, "scalar"), (9, 1, "scalar")]
 HELD_BACK = {(2, 5), (2, 6), (2, 7)}
@@ -18,7 +19,7 @@ TURN_RUNS = [(0, 2, 5), (2, 2, 6), (4, 2, 7), (6, 2, 5), (8, 1, 2), (9, 1, 4)]
 Y_BANK = {0: 6, 4: 3, 8: 0, 9: 1}
 CAST_BEHIND = {4: "hidden_3", 5: "hidden_4", 6: "hidden_5"}
 H_TILES = [(0, 4, "h_grouped_0"), (4, 4, "grouped_7"), (8, 2, "h_grouped_8")]
-CODE_TILES = {6: (6, 2, "hidden_7"), 7: (6, 2, "hidden_7")}
+CODE_TILES = {6: (6, 2, "hidden_7_0"), 7: (6, 2, "hidden_7_0")}
 LATE_REST = {2, 4}
 GATE_CUTS = [0, 128, 640, 1024, S]
 OUT_PIECES = [(0, 448), (448, 192)]
@@ -73,14 +74,14 @@ def tile_moe_pre_mlp_silu_kernel(
         ident = held.tile([P, P], F32, name="ident")
         y_sb = held.tile([P, S], F32, name="y_sb")
 
+        for j in range(PACK):
+            nc.vector.memset(x_sb[0, j][:, T:], 0.0)
         nc.vector.memset(w1_plane[:].rearrange("p a i -> p (a i)").bitcast(I32), 0)
         nc.vector.memset(w2_plane[:].rearrange("p a i -> p (a i)").bitcast(I32), 0)
-        for s in range(PASSES):
-            if s == 1:
-                make_identity(nc, ident[:])
+        make_identity(nc, ident[:])
+        for s in range(1, PASSES):
             for j in range(PACK):
-                if width[s] > T:
-                    nc.gpsimd.memset(x_sb[s, j][:, T:], 0.0)
+                nc.gpsimd.memset(x_sb[s, j][:, T:], 0.0)
 
         def load_x(s, planes):
             for j in planes:
@@ -131,13 +132,45 @@ def tile_moe_pre_mlp_silu_kernel(
 
         def cast(k):
             u0, units, s = STEPS[k]
-            grouped[k] = held.tile([P, units * UNIT, PACK], BF16, name=f"grouped_{k}", tag=CAST_BEHIND.get(k, f"grouped_{k}"), align_bytes=64)
-            for a, m in chunks(units):
+            if k == 0:
+                grouped["both"] = held.tile([P, 2 * units * UNIT, PACK], BF16, name="grouped_both", align_bytes=64)
+            if k < 2:
+                grouped[k] = grouped["both"][:, k * units * UNIT : (k + 1) * units * UNIT, :]
+            else:
+                grouped[k] = held.tile([P, units * UNIT, PACK], BF16, name=f"grouped_{k}", tag=CAST_BEHIND.get(k, f"grouped_{k}"), align_bytes=64)
+            for a, m in [(0, units)] if k < 2 else chunks(units):
                 cols = slice(a * UNIT, (a + m) * UNIT)
                 nc.scalar.copy(
                     grouped[k][:, cols, :].rearrange("p (c i) t -> p c t i", i=4),
                     picked[k][:, :, cols].rearrange("p t (c i) -> p c t i", i=4),
                 )
+
+        def first_two():
+            units = STEPS[0][1]
+            codes = held.tile([P, 2 * units * UNIT], U32, name="codes_both", align_bytes=64)
+            scales = held.tile([P, 2 * units * UNIT], U8, name="scales_both", align_bytes=64)
+            for a, m in [(0, 8), (8, 2)]:
+                cols = slice(a * UNIT, (a + m) * UNIT)
+                nc.vector.quantize_mx(codes[:, cols].bitcast(FP8X4), scales[:, cols], grouped["both"][:, cols, :].rearrange("p c t -> p (c t)"))
+                for b in range(a, a + m):
+                    one = slice(b * UNIT, (b + 1) * UNIT)
+                    multiply(b % units, STEPS[b // units][2], codes[:, one], scales[:, one])
+
+        def multiply(u, s, words, plane):
+            n = done.get(u, 0)
+            e = u * UNIT // C
+            if n == 0:
+                acc[u] = psum.tile([P, H], F32, name=f"acc_{u}", tag=f"bank_{ACC_BANK[u]}")
+            nc.tensor.matmul_mx(
+                out=acc[u][:],
+                lhsT=words.bitcast(FP8X4),
+                lhsT_scale=plane,
+                rhs=w1_sb[e][:, s, :].bitcast(FP4X4),
+                rhs_scale=w1_plane[:, e * PASSES + s, :],
+                start=(n == 0),
+                stop=(n == PASSES - 1),
+            )
+            done[u] = n + 1
 
         def first_layer(k, parts):
             u0, units, s = STEPS[k]
@@ -154,40 +187,30 @@ def tile_moe_pre_mlp_silu_kernel(
                 nc.vector.quantize_mx(codes[:, cols].bitcast(FP8X4), scales[:, cols], grouped[k][:, cols, :].rearrange("p c t -> p (c t)"))
                 for b in range(a, a + m):
                     u = u0 + b
-                    e = u * UNIT // C
                     one = slice(b * UNIT, (b + 1) * UNIT)
                     waiting.setdefault(u, []).append((s, codes[:, one], scales[:, one]))
                     if (k, u) in HELD_BACK:
                         continue
                     for s1, words, plane in waiting.pop(u):
-                        n = done.get(u, 0)
-                        if n == 0:
-                            acc[u] = psum.tile([P, H], F32, name=f"acc_{u}", tag=f"bank_{ACC_BANK[u]}")
-                        nc.tensor.matmul_mx(
-                            out=acc[u][:],
-                            lhsT=words.bitcast(FP8X4),
-                            lhsT_scale=plane,
-                            rhs=w1_sb[e][:, s1, :].bitcast(FP4X4),
-                            rhs_scale=w1_plane[:, e * PASSES + s1, :],
-                            start=(n == 0),
-                            stop=(n == PASSES - 1),
-                        )
-                        done[u] = n + 1
+                        multiply(u, s1, words, plane)
 
         def silu(u):
-            hidden[u] = held.tile([P, 2, P, 2], BF16, name=f"hidden_{u}", align_bytes=64)
             sums = acc[u][:].rearrange("c (p v d) -> c v p d", v=2, d=2)
-            halves = [slice(0, 1), slice(1, 2)] if u == S // UNIT - 1 else [slice(0, 2)]
-            for half in halves:
-                nc.scalar.activation(hidden[u][:, half], sums[:, half], SILU)
+            if u in HALVED:
+                hidden[u] = [held.tile([P, P, 2], BF16, name=f"hidden_{u}_{v}", align_bytes=64)[:] for v in range(2)]
+                for v in range(2):
+                    nc.scalar.activation(hidden[u][v], sums[:, v], SILU)
+            else:
+                whole = held.tile([P, 2, P, 2], BF16, name=f"hidden_{u}", align_bytes=64)
+                nc.scalar.activation(whole[:], sums, SILU)
+                hidden[u] = [whole[:, v] for v in range(2)]
 
         def turn(u):
-            pairs = hidden[u][:].rearrange("c v p d -> c (v p d)").bitcast(F32)
             first, count, bank = [run for run in TURN_RUNS if run[0] <= u][-1]
             if u == first:
                 turned[first] = psum.tile([P, count, 2, UNIT], F32, name=f"turned_{u}", tag=f"bank_{bank}")
             for v in range(2):
-                nc.tensor.transpose(turned[first][:, u - first, v, :], pairs[:, v * P : (v + 1) * P], ident[:])
+                nc.tensor.transpose(turned[first][:, u - first, v, :], hidden[u][v].rearrange("c p d -> c (p d)").bitcast(F32), ident[:])
 
         def weave(first, count, engine):
             words = h_rows(first, count).bitcast(F32)
@@ -232,11 +255,12 @@ def tile_moe_pre_mlp_silu_kernel(
         def behind(k):
             first_layer(k - 1, slice(0, 1) if k - 1 in LATE_REST else slice(None))
 
-        step(0)
-        cast(0)
-        for k in range(1, 4):
+        for k in range(4):
             step(k)
-            behind(k)
+            if k == 2:
+                first_two()
+            if k == 3:
+                behind(k)
             cast(k)
         step(4)
         for u in range(5):
@@ -256,15 +280,15 @@ def tile_moe_pre_mlp_silu_kernel(
             step(k)
             behind(k)
             cast(k)
+        early_scales = held.tile([P, S], U8, name="early_scales", tag="hidden_7_1", align_bytes=64)
+        second_layer(0, 2, early_scales)
         first_layer(last, slice(None))
         for u in (8, 9):
             silu(u)
         for u in (8, 9):
             turn(u)
             weave(u, 1, "scalar")
-        early_scales = held.tile([P, S], U8, name="early_scales", tag=f"x_{STEPS[last][2]}_{PACK - 1}", align_bytes=64)
         late_scales = held.tile([P, S], U8, name="late_scales", tag=f"scales_{last}", align_bytes=64)
-        second_layer(0, 2, early_scales)
         for u in (4, 6):
             weave(u, 2, "vector")
         for u0, units in [(2, 2), (4, 4), (8, 1), (9, 1)]:

@@ -65,8 +65,9 @@ def tile_moe_pre_mlp_silu_kernel(
         x_rows = xT.rearrange("(s p j) t -> s j p t", p=P, j=PACK)
         widest = [max(units * UNIT for u0, units, s in STEPS if s == a) for a in range(PASSES)]
         width = [T if widest[s] < T else widest[s] + SPARE for s in range(PASSES)]
-        x_sb = {(s, j): held.tile([P, width[s]], F32, name=f"x_{s}_{j}", align_bytes=64) for s in range(PASSES) for j in range(PACK)}
-        gate_sb = held.tile([P, S], F32, name="gate_sb")
+        x_sb = {(s, j): held.tile([P, width[s]], F32, name=f"x_{s}_{j}", align_bytes=256) for s in range(PASSES) for j in range(PACK)}
+        gate_padded = held.tile([P, S + 32], F32, name="gate_sb", align_bytes=256)
+        gate_sb = gate_padded[:, 32:]
         w1_sb = [held.tile([P, PASSES, 2 * H], U8, name=f"w1_{e}", align_bytes=64) for e in range(E)]
         w2_sb = held.tile([P, E, 2 * N], U8, name="w2_sb", align_bytes=64)
         w1_plane = held.tile([P, E * PASSES, H], U8, name="w1_plane", align_bytes=64)
@@ -124,7 +125,7 @@ def tile_moe_pre_mlp_silu_kernel(
             u0, units, s = STEPS[k]
             lo, hi = u0 * UNIT, (u0 + units) * UNIT
             if j == 0:
-                picked[k] = ring.tile([P, PACK, hi - lo], F32, name=f"picked_{k}", tag="picked", bufs=2)
+                picked[k] = ring.tile([P, PACK, hi - lo], F32, name=f"picked_{k}", tag="picked", bufs=2, align_bytes=256)
             ends = GATE_CUTS[:3] if (k, j) == (0, 0) else [lo, hi]
             for a, b in zip(ends, ends[1:]):
                 window = x_sb[s, j][:].indirect(offs_sb[:, a // 16 : b // 16])

@@ -9,20 +9,21 @@ P = 128
 PACK = 4
 PASSES = K // (P * PACK)
 UNIT = 128
-SPARE = 16
-HALVED = (7, 9)
+PER_COLUMN = 16
+
 STEPS = [(0, 5, 0), (0, 5, 1), (0, 8, 2), (5, 3, 0), (5, 5, 1), (8, 2, 0), (8, 1, 2), (9, 1, 2)]
-Y_RUNS = [(0, 4, "scalar"), (4, 4, "vector"), (8, 1, "scalar"), (9, 1, "scalar")]
-HELD_BACK = {(2, 5), (2, 6), (2, 7)}
-ACC_BANK = [0, 1, 2, 3, 4, 4, 6, 3, 0, 1]
-TURN_RUNS = [(0, 2, 5), (2, 2, 6), (4, 2, 7), (6, 2, 5), (8, 1, 2), (9, 1, 4)]
-Y_BANK = {0: 6, 4: 3, 8: 0, 9: 1}
-CAST_BEHIND = {4: "hidden_3", 5: "hidden_4", 6: "hidden_5"}
-H_TILES = [(0, 4, "h_grouped_0"), (4, 4, "grouped_7"), (8, 2, "h_grouped_8")]
-CODE_TILES = {6: (6, 2, "hidden_7_0"), 7: (6, 2, "hidden_7_0")}
-LATE_REST = {2, 4}
-GATE_CUTS = [0, 128, 640, 1024, S]
+LAST = len(STEPS) - 1
+FIRST_GROUP, SECOND_GROUP, THIRD_GROUP = range(0, 5), range(5, 8), range(8, 10)
+WIDE_STEPS = (2, 4)
+SPARE = 16
+GATE_CUTS = [0, 192, 640, 1024, S]
+GATE_SHIFT = 32
 OUT_PIECES = [(0, 448), (448, 192)]
+
+SUM_BANK = [0, 1, 2, 3, 4, 4, 6, 3, 0, 1]
+TURN_RUNS = [(0, 2, 5), (2, 2, 6), (4, 2, 7), (6, 2, 5), (8, 1, 2), (9, 1, 4)]
+RESULT_RUNS = [(0, 4, 6), (4, 4, 3), (8, 1, 0), (9, 1, 1)]
+HALVED = (7, 9)
 
 FLOPS = 2 * S * (K * H + H * N)
 BYTES = 4 * K * T + E * (K * H + H * N) // 2 + E * (K * H + H * N) // 32 + 4 * S + 2 * P * (S + 2 * T) // 16 + 4 * N * T
@@ -40,13 +41,21 @@ ADD = mybir.AluOpType.add
 SILU = mybir.ActivationFunctionType.Silu
 
 
-def chunks(units):
-    runs, a = [], 0
-    while a < units:
-        m = max(w for w in (4, 2, 1) if w <= units - a)
-        runs.append((a, m))
-        a += m
+def chunks(units, widest):
+    runs, done = [], 0
+    while done < units:
+        size = max(w for w in (8, 4, 2, 1) if w <= min(widest, units - done))
+        runs.append((done, size))
+        done += size
     return runs
+
+
+def slots(first, units):
+    return slice(first * UNIT, (first + units) * UNIT)
+
+
+def run_of(runs, u):
+    return [run for run in runs if run[0] <= u][-1]
 
 
 def tile_moe_pre_mlp_silu_kernel(
@@ -55,254 +64,255 @@ def tile_moe_pre_mlp_silu_kernel(
     nc = tc.nc
     with ExitStack() as ctx:
         held = ctx.enter_context(tc.tile_pool(name="held", bufs=1))
-        ring = ctx.enter_context(tc.tile_pool(name="ring", bufs=3))
+        ring = ctx.enter_context(tc.tile_pool(name="ring", bufs=2))
         psum = ctx.enter_context(tc.psum_pool(name="psum", bufs=1))
 
-        last = len(STEPS) - 1
-        offs_sb = held.tile([P, S // 16], U16, name="offs_sb")
-        pos1_sb = held.tile([P, T // 16], U16, name="pos1_sb")
-        pos2_sb = held.tile([P, T // 16], U16, name="pos2_sb")
-        x_rows = xT.rearrange("(s p j) t -> s j p t", p=P, j=PACK)
-        widest = [max(units * UNIT for u0, units, s in STEPS if s == a) for a in range(PASSES)]
-        width = [T if widest[s] < T else widest[s] + SPARE for s in range(PASSES)]
-        x_sb = {(s, j): held.tile([P, width[s]], F32, name=f"x_{s}_{j}", align_bytes=256) for s in range(PASSES) for j in range(PACK)}
-        gate_padded = held.tile([P, S + 32], F32, name="gate_sb", align_bytes=256)
-        gate_sb = gate_padded[:, 32:]
+        offs_sb = held.tile([P, S // PER_COLUMN], U16, name="offs_sb")
+        pos1_sb = held.tile([P, T // PER_COLUMN], U16, name="pos1_sb")
+        pos2_sb = held.tile([P, T // PER_COLUMN], U16, name="pos2_sb")
+        width = [SPARE + max(units * UNIT for first, units, s in STEPS if s == a) for a in range(PASSES)]
+        plane = {
+            (s, t): held.tile([P, width[s]], F32, name=f"plane_{s}_{t}", align_bytes=256)
+            for s in range(PASSES)
+            for t in range(PACK)
+        }
+        gate_tile = held.tile([P, GATE_SHIFT + S], F32, name="gate_tile", align_bytes=256)
+        gate_sb = gate_tile[:, GATE_SHIFT:]
         w1_sb = [held.tile([P, PASSES, 2 * H], U8, name=f"w1_{e}", align_bytes=64) for e in range(E)]
         w2_sb = held.tile([P, E, 2 * N], U8, name="w2_sb", align_bytes=64)
-        w1_plane = held.tile([P, E * PASSES, H], U8, name="w1_plane", align_bytes=64)
-        w2_plane = held.tile([P, E, N], U8, name="w2_plane", align_bytes=64)
+        w1_scale_sb = held.tile([P, E * PASSES, H], U8, name="w1_scale_sb", align_bytes=64)
+        w2_scale_sb = held.tile([P, E, N], U8, name="w2_scale_sb", align_bytes=64)
         ident = held.tile([P, P], F32, name="ident")
         y_sb = held.tile([P, S], F32, name="y_sb")
 
-        for j in range(PACK):
-            nc.vector.memset(x_sb[0, j][:, T:], 0.0)
-        nc.vector.memset(w1_plane[:].rearrange("p a i -> p (a i)").bitcast(I32), 0)
-        nc.vector.memset(w2_plane[:].rearrange("p a i -> p (a i)").bitcast(I32), 0)
+        for t in range(PACK):
+            nc.vector.memset(plane[0, t][:, T:], 0.0)
+        nc.vector.memset(w1_scale_sb[:].rearrange("p a i -> p (a i)").bitcast(I32), 0)
+        nc.vector.memset(w2_scale_sb[:].rearrange("p a i -> p (a i)").bitcast(I32), 0)
         make_identity(nc, ident[:])
         for s in range(1, PASSES):
-            for j in range(PACK):
-                nc.gpsimd.memset(x_sb[s, j][:, T:], 0.0)
+            for t in range(PACK):
+                nc.gpsimd.memset(plane[s, t][:, T:], 0.0)
 
-        def load_x(s, planes):
-            for j in planes:
-                nc.sync.dma_start(x_sb[s, j][:, 0:T], x_rows[s, j])
+        x_rows = xT.rearrange("(s p t) c -> s t p c", p=P, t=PACK)
 
-        def load_gate(queue, c):
-            cols = slice(GATE_CUTS[c], GATE_CUTS[c + 1])
+        def load_planes(s, rows):
+            for t in rows:
+                nc.sync.dma_start(plane[s, t][:, 0:T], x_rows[s, t])
+
+        def load_gate(queue, piece):
+            cols = slice(GATE_CUTS[piece], GATE_CUTS[piece + 1])
             queue.dma_start(gate_sb[:, cols], gate[0:P, cols])
 
-        def load_w1(e):
-            nc.sync.dma_start(w1_sb[e][:].bitcast(I32), w1_words[e].rearrange("s p b -> p s b").bitcast(I32))
-
-        def load_plane(plane, scales, lo, hi):
+        def load_scales(scale_sb, scales):
             rows = scales.rearrange("e s q i -> q (e s) i").bitcast(I32)
             for quad in range(4):
-                nc.sync.dma_start(plane[32 * quad : 32 * quad + 4, lo:hi, :].bitcast(I32), rows[4 * quad : 4 * quad + 4, lo:hi, :])
+                nc.sync.dma_start(scale_sb[32 * quad : 32 * quad + 4].bitcast(I32), rows[4 * quad : 4 * quad + 4])
 
-        load_x(0, [0])
+        load_planes(0, [0])
         nc.sync.dma_start(offs_sb[:], offs)
         load_gate(nc.scalar, 0)
-        load_gate(nc.sync, 1)
-        load_x(0, [1, 2, 3])
-        load_x(1, range(PACK))
+        load_gate(nc.scalar, 1)
+        load_planes(0, range(1, PACK))
+        load_planes(1, range(PACK))
         load_gate(nc.sync, 2)
-        load_x(2, range(PACK))
+        load_planes(2, range(PACK))
         load_gate(nc.sync, 3)
-        load_plane(w1_plane, w1_scales, 0, E * PASSES)
-        load_plane(w2_plane, w2_scales, 0, E)
+        load_scales(w1_scale_sb, w1_scales)
+        load_scales(w2_scale_sb, w2_scales)
         for e in range(E):
-            load_w1(e)
+            nc.sync.dma_start(w1_sb[e][:].bitcast(I32), w1_words[e].rearrange("s p b -> p s b").bitcast(I32))
         nc.sync.dma_start(w2_sb[:].bitcast(I32), w2_words.rearrange("e s p b -> p (e s) b").bitcast(I32))
         nc.sync.dma_start(pos1_sb[:], pos1)
         nc.sync.dma_start(pos2_sb[:], pos2)
 
-        acc, picked, grouped, y_ps, waiting, done = {}, {}, {}, {}, {}, {}
-        hidden, turned, h_grouped, coded, scaled = {}, {}, {}, {}, {}
+        picked, rounded, x_codes, x_scales = {}, {}, {}, {}
+        sums, passes_done, waiting, hidden = {}, {}, {}, {}
+        turned, h_rounded, results = {}, {}, {}
         h_codes = held.tile([P, S], U32, name="h_codes", align_bytes=64)
 
-        def gather(k, j):
-            u0, units, s = STEPS[k]
-            lo, hi = u0 * UNIT, (u0 + units) * UNIT
-            if j == 0:
-                picked[k] = ring.tile([P, PACK, hi - lo], F32, name=f"picked_{k}", tag="picked", bufs=2, align_bytes=256)
-            ends = GATE_CUTS[:3] if (k, j) == (0, 0) else [lo, hi]
-            for a, b in zip(ends, ends[1:]):
-                window = x_sb[s, j][:].indirect(offs_sb[:, a // 16 : b // 16])
-                nc.vector.tensor_tensor(picked[k][:, j, a - lo : b - lo], window, gate_sb[:, a:b], MULT)
+        def gather(k):
+            first, units, s = STEPS[k]
+            lo, hi = first * UNIT, (first + units) * UNIT
+            picked[k] = ring.tile([P, PACK, hi - lo], F32, name=f"picked_{k}", tag="picked", align_bytes=256)
+            for t in range(PACK):
+                ends = GATE_CUTS[:3] if (k, t) == (0, 0) else [lo, hi]
+                for a, b in zip(ends, ends[1:]):
+                    tokens = plane[s, t][:].indirect(offs_sb[:, a // PER_COLUMN : b // PER_COLUMN])
+                    nc.vector.tensor_tensor(picked[k][:, t, a - lo : b - lo], tokens, gate_sb[:, a:b], MULT)
+                if t == 0 and k - 2 in WIDE_STEPS:
+                    first_layer(k - 2, slice(1, None))
 
-        def cast(k):
-            u0, units, s = STEPS[k]
-            if k == 0:
-                grouped["both"] = held.tile([P, 2 * units * UNIT, PACK], BF16, name="grouped_both", align_bytes=64)
-            if k < 2:
-                grouped[k] = grouped["both"][:, k * units * UNIT : (k + 1) * units * UNIT, :]
-            else:
-                grouped[k] = held.tile([P, units * UNIT, PACK], BF16, name=f"grouped_{k}", tag=CAST_BEHIND.get(k, f"grouped_{k}"), align_bytes=64)
-            for a, m in [(0, units)] if k < 2 else chunks(units):
-                cols = slice(a * UNIT, (a + m) * UNIT)
+        def round_rows(k, into, runs):
+            rounded[k] = into
+            for a, units in runs:
                 nc.scalar.copy(
-                    grouped[k][:, cols, :].rearrange("p (c i) t -> p c t i", i=4),
-                    picked[k][:, :, cols].rearrange("p t (c i) -> p c t i", i=4),
+                    into[:, slots(a, units), :].rearrange("p (c i) t -> p c t i", i=4),
+                    picked[k][:, :, slots(a, units)].rearrange("p t (c i) -> p c t i", i=4),
                 )
 
-        def first_two():
-            units = STEPS[0][1]
-            codes = held.tile([P, 2 * units * UNIT], U32, name="codes_both", align_bytes=64)
-            scales = held.tile([P, 2 * units * UNIT], U8, name="scales_both", align_bytes=64)
-            for a, m in [(0, 8), (8, 2)]:
-                cols = slice(a * UNIT, (a + m) * UNIT)
-                nc.vector.quantize_mx(codes[:, cols].bitcast(FP8X4), scales[:, cols], grouped["both"][:, cols, :].rearrange("p c t -> p (c t)"))
-                for b in range(a, a + m):
-                    one = slice(b * UNIT, (b + 1) * UNIT)
-                    multiply(b % units, STEPS[b // units][2], codes[:, one], scales[:, one])
+        def round_step(k, tag):
+            units = STEPS[k][1]
+            into = held.tile([P, units * UNIT, PACK], BF16, name=f"rounded_{k}", tag=tag, align_bytes=64)
+            round_rows(k, into, chunks(units, 4))
 
-        def multiply(u, s, words, plane):
-            n = done.get(u, 0)
-            e = u * UNIT // C
-            if n == 0:
-                acc[u] = psum.tile([P, H], F32, name=f"acc_{u}", tag=f"bank_{ACC_BANK[u]}")
+        def multiply(u, s, codes, scales):
+            e, done = u * UNIT // C, passes_done.get(u, 0)
+            if done == 0:
+                sums[u] = psum.tile([P, H], F32, name=f"sums_{u}", tag=f"bank_{SUM_BANK[u]}")
             nc.tensor.matmul_mx(
-                out=acc[u][:],
-                lhsT=words.bitcast(FP8X4),
-                lhsT_scale=plane,
+                out=sums[u][:],
+                lhsT=codes.bitcast(FP8X4),
+                lhsT_scale=scales,
                 rhs=w1_sb[e][:, s, :].bitcast(FP4X4),
-                rhs_scale=w1_plane[:, e * PASSES + s, :],
-                start=(n == 0),
-                stop=(n == PASSES - 1),
+                rhs_scale=w1_scale_sb[:, e * PASSES + s, :],
+                start=(done == 0),
+                stop=(done == PASSES - 1),
             )
-            done[u] = n + 1
+            passes_done[u] = done + 1
+
+        def quantise(codes, scales, values):
+            nc.vector.quantize_mx(codes.bitcast(FP8X4), scales, values.rearrange("p c t -> p (c t)"))
+
+        def first_layer_of_two_steps(values):
+            count = 2 * len(FIRST_GROUP)
+            codes = held.tile([P, count * UNIT], U32, name="x_codes_first", align_bytes=64)
+            scales = held.tile([P, count * UNIT], U8, name="x_scales_first", align_bytes=64)
+            for a, units in chunks(count, 8):
+                quantise(codes[:, slots(a, units)], scales[:, slots(a, units)], values[:, slots(a, units), :])
+                for b in range(a, a + units):
+                    k, u = divmod(b, len(FIRST_GROUP))
+                    multiply(u, STEPS[k][2], codes[:, slots(b, 1)], scales[:, slots(b, 1)])
 
         def first_layer(k, parts):
-            u0, units, s = STEPS[k]
-            first, count, tag = CODE_TILES.get(k, (k, units, f"codes_{k}"))
-            if first not in coded:
-                coded[first] = held.tile([P, count * UNIT], U32, name=f"codes_{first}", tag=tag, align_bytes=64)
-            skip = (u0 - STEPS[first][0]) * UNIT
-            codes = coded[first][:, skip : skip + units * UNIT]
-            if k not in scaled:
-                scaled[k] = held.tile([P, units * UNIT], U8, name=f"scales_{k}", align_bytes=64)
-            scales = scaled[k]
-            for a, m in chunks(units)[parts]:
-                cols = slice(a * UNIT, (a + m) * UNIT)
-                nc.vector.quantize_mx(codes[:, cols].bitcast(FP8X4), scales[:, cols], grouped[k][:, cols, :].rearrange("p c t -> p (c t)"))
-                for b in range(a, a + m):
-                    u = u0 + b
-                    one = slice(b * UNIT, (b + 1) * UNIT)
-                    waiting.setdefault(u, []).append((s, codes[:, one], scales[:, one]))
-                    if (k, u) in HELD_BACK:
-                        continue
-                    for s1, words, plane in waiting.pop(u):
-                        multiply(u, s1, words, plane)
+            first, units, s = STEPS[k]
+            if k not in x_codes:
+                x_codes[k] = held.tile([P, units * UNIT], U32, name=f"x_codes_{k}", align_bytes=64)[:]
+            if k not in x_scales:
+                x_scales[k] = held.tile([P, units * UNIT], U8, name=f"x_scales_{k}", align_bytes=64)
+            for a, size in chunks(units, 4)[parts]:
+                quantise(x_codes[k][:, slots(a, size)], x_scales[k][:, slots(a, size)], rounded[k][:, slots(a, size), :])
+                for b in range(a, a + size):
+                    u = first + b
+                    waiting.setdefault(u, []).append((s, x_codes[k][:, slots(b, 1)], x_scales[k][:, slots(b, 1)]))
+                    if u not in SECOND_GROUP or len(waiting[u]) + passes_done.get(u, 0) > 1:
+                        for queued in waiting.pop(u):
+                            multiply(u, *queued)
+
+        def first_layer_behind(k):
+            first_layer(k - 1, slice(0, 1) if k - 1 in WIDE_STEPS else slice(None))
 
         def silu(u):
-            sums = acc[u][:].rearrange("c (p v d) -> c v p d", v=2, d=2)
+            by_half = sums[u][:].rearrange("c (p v d) -> c v p d", v=2, d=2)
             if u in HALVED:
                 hidden[u] = [held.tile([P, P, 2], BF16, name=f"hidden_{u}_{v}", align_bytes=64)[:] for v in range(2)]
                 for v in range(2):
-                    nc.scalar.activation(hidden[u][v], sums[:, v], SILU)
+                    nc.scalar.activation(hidden[u][v], by_half[:, v], SILU)
             else:
                 whole = held.tile([P, 2, P, 2], BF16, name=f"hidden_{u}", align_bytes=64)
-                nc.scalar.activation(whole[:], sums, SILU)
+                nc.scalar.activation(whole[:], by_half, SILU)
                 hidden[u] = [whole[:, v] for v in range(2)]
 
         def turn(u):
-            first, count, bank = [run for run in TURN_RUNS if run[0] <= u][-1]
+            first, units, bank = run_of(TURN_RUNS, u)
             if u == first:
-                turned[first] = psum.tile([P, count, 2, UNIT], F32, name=f"turned_{u}", tag=f"bank_{bank}")
+                turned[first] = psum.tile([P, units, 2, UNIT], F32, name=f"turned_{first}", tag=f"bank_{bank}")
             for v in range(2):
-                nc.tensor.transpose(turned[first][:, u - first, v, :], hidden[u][v].rearrange("c p d -> c (p d)").bitcast(F32), ident[:])
-
-        def weave(first, count, engine):
-            words = h_rows(first, count).bitcast(F32)
-            copy = nc.scalar.copy if engine == "scalar" else nc.vector.tensor_copy
-            copy(words.rearrange("p (u c v) -> p u c v", u=count, v=2), turned[first][:].rearrange("p u v c -> p u c v"))
+                pairs = hidden[u][v].rearrange("c p d -> c (p d)").bitcast(F32)
+                nc.tensor.transpose(turned[first][:, u - first, v, :], pairs, ident[:])
 
         def h_rows(u, units):
-            first, count, tag = [run for run in H_TILES if run[0] <= u][-1]
-            if first not in h_grouped:
-                h_grouped[first] = held.tile([P, count * UNIT * PACK], BF16, name=f"h_grouped_{first}", tag=tag, align_bytes=64)
-            return h_grouped[first][:, (u - first) * UNIT * PACK : (u - first + units) * UNIT * PACK]
+            first, count, tag = run_of([(0, 4, "h_rounded_0"), (4, 4, f"rounded_{LAST}"), (8, 2, "h_rounded_8")], u)
+            if first not in h_rounded:
+                h_rounded[first] = held.tile([P, count * UNIT * PACK], BF16, name=f"h_rounded_{first}", tag=tag, align_bytes=64)
+            return h_rounded[first][:, (u - first) * UNIT * PACK : (u - first + units) * UNIT * PACK]
 
-        def second_layer(u0, units, h_scales):
-            lo, hi = u0 * UNIT, (u0 + units) * UNIT
-            nc.vector.quantize_mx(h_codes[:, lo:hi].bitcast(FP8X4), h_scales[:, lo:hi], h_rows(u0, units))
-            first, count, engine = [run for run in Y_RUNS if run[0] <= u0][-1]
-            if u0 == first:
-                y_ps[first] = psum.tile([P, count * UNIT], F32, name=f"y_{u0}", tag=f"bank_{Y_BANK[first]}")
-            base = first * UNIT
-            cuts = sorted({lo, hi} | {a for a in range(0, S, C) if lo < a < hi})
-            for a, b in zip(cuts, cuts[1:]):
+        def weave(first, copy):
+            units = run_of(TURN_RUNS, first)[1]
+            words = h_rows(first, units).bitcast(F32).rearrange("p (u c v) -> p u c v", u=units, v=2)
+            copy(words, turned[first][:].rearrange("p u v c -> p u c v"))
+
+        def second_layer(u, units, h_scales):
+            cols = slots(u, units)
+            nc.vector.quantize_mx(h_codes[:, cols].bitcast(FP8X4), h_scales[:, cols], h_rows(u, units))
+            first, count, bank = run_of(RESULT_RUNS, u)
+            if u == first:
+                results[first] = psum.tile([P, count * UNIT], F32, name=f"results_{first}", tag=f"bank_{bank}")
+            for a in range(cols.start, cols.stop, C):
+                b = min(a + C, cols.stop)
                 nc.tensor.matmul_mx(
-                    out=y_ps[first][:, a - base : b - base],
+                    out=results[first][:, a - first * UNIT : b - first * UNIT],
                     lhsT=w2_sb[:, a // C, :].bitcast(FP4X4),
-                    lhsT_scale=w2_plane[:, a // C, :],
+                    lhsT_scale=w2_scale_sb[:, a // C, :],
                     rhs=h_codes[:, a:b].bitcast(FP8X4),
                     rhs_scale=h_scales[:, a:b],
                     start=True,
                     stop=True,
                 )
 
-        def fetch_sums(first, count, engine):
-            copy = nc.scalar.copy if engine == "scalar" else nc.vector.tensor_copy
-            copy(y_sb[:, first * UNIT : (first + count) * UNIT], y_ps[first][:])
+        group_units = len(FIRST_GROUP)
+        gather(0)
+        two_steps = held.tile([P, 2 * group_units * UNIT, PACK], BF16, name="two_steps", align_bytes=64)
+        round_rows(0, two_steps[:, slots(0, group_units), :], [(0, group_units)])
+        gather(1)
+        round_rows(1, two_steps[:, slots(group_units, group_units), :], [(0, group_units)])
+        gather(2)
+        first_layer_of_two_steps(two_steps)
+        round_step(2, "rounded_2")
+        gather(3)
+        first_layer_behind(3)
+        round_step(3, "rounded_3")
 
-        def step(k):
-            for j in range(PACK):
-                gather(k, j)
-                if j == 0 and k - 2 in LATE_REST:
-                    first_layer(k - 2, slice(1, None))
-
-        def behind(k):
-            first_layer(k - 1, slice(0, 1) if k - 1 in LATE_REST else slice(None))
-
-        for k in range(4):
-            step(k)
-            if k == 2:
-                first_two()
-            if k == 3:
-                behind(k)
-            cast(k)
-        step(4)
-        for u in range(5):
+        gather(4)
+        for u in FIRST_GROUP:
             silu(u)
             turn(u)
-            if u in (1, 3):
-                weave(u - 1, 2, "scalar")
-        behind(4)
-        cast(4)
-        step(5)
-        behind(5)
-        cast(5)
-        for u in (5, 6, 7):
+            if u % 2 == 1:
+                weave(u - 1, nc.scalar.copy)
+        first_layer_behind(4)
+        round_step(4, "hidden_3")
+        gather(5)
+        first_layer_behind(5)
+        round_step(5, "hidden_4")
+
+        for u in SECOND_GROUP:
             silu(u)
             turn(u)
-        for k in (6, 7):
-            step(k)
-            behind(k)
-            cast(k)
+        gather(6)
+        first_layer_behind(6)
+        round_step(6, "hidden_5")
+        gather(LAST)
+
+        last_codes = held.tile([P, 2 * UNIT], U32, name="last_codes", tag="hidden_7_0", align_bytes=64)
+        x_codes[LAST - 1], x_codes[LAST] = last_codes[:, slots(0, 1)], last_codes[:, slots(1, 1)]
+        first_layer_behind(LAST)
+        round_step(LAST, f"rounded_{LAST}")
+
         early_scales = held.tile([P, S], U8, name="early_scales", tag="hidden_7_1", align_bytes=64)
         second_layer(0, 2, early_scales)
-        first_layer(last, slice(None))
-        for u in (8, 9):
+        first_layer(LAST, slice(None))
+        for u in THIRD_GROUP:
             silu(u)
-        for u in (8, 9):
+        for u in THIRD_GROUP:
             turn(u)
-            weave(u, 1, "scalar")
-        late_scales = held.tile([P, S], U8, name="late_scales", tag=f"scales_{last}", align_bytes=64)
-        for u in (4, 6):
-            weave(u, 2, "vector")
-        for u0, units in [(2, 2), (4, 4), (8, 1), (9, 1)]:
-            second_layer(u0, units, late_scales)
-        for run in Y_RUNS:
-            fetch_sums(*run)
+            weave(u, nc.scalar.copy)
+        late_scales = held.tile([P, S], U8, name="late_scales", tag=f"x_scales_{LAST}", align_bytes=64)
+        for first in (4, 6):
+            weave(first, nc.vector.tensor_copy)
+        for u, units in [(2, 2), (4, 4), (8, 1), (9, 1)]:
+            second_layer(u, units, late_scales)
 
-        fetched = []
+        for first, units, bank in RESULT_RUNS:
+            copy = nc.vector.tensor_copy if first == RESULT_RUNS[1][0] else nc.scalar.copy
+            copy(y_sb[:, slots(first, units)], results[first][:])
+
+        by_pos1 = []
         for lo, n in OUT_PIECES:
             one = held.tile([P, n], F32, name=f"one_{lo}")
-            nc.vector.tensor_copy(one[:], y_sb[:].indirect(pos1_sb[:, lo // 16 : (lo + n) // 16]))
-            fetched.append((lo, n, one))
-        for lo, n, one in fetched:
+            nc.vector.tensor_copy(one[:], y_sb[:].indirect(pos1_sb[:, lo // PER_COLUMN : (lo + n) // PER_COLUMN]))
+            by_pos1.append(one)
+        for (lo, n), one in zip(OUT_PIECES, by_pos1):
             both = held.tile([P, n], F32, name=f"both_{lo}")
-            nc.vector.tensor_tensor(both[:], y_sb[:].indirect(pos2_sb[:, lo // 16 : (lo + n) // 16]), one[:], ADD)
+            other = y_sb[:].indirect(pos2_sb[:, lo // PER_COLUMN : (lo + n) // PER_COLUMN])
+            nc.vector.tensor_tensor(both[:], other, one[:], ADD)
             nc.sync.dma_start(out[:, lo : lo + n], both[:])

@@ -112,7 +112,7 @@ def tile_moe_pre_mlp_silu_kernel(
         load_planes(0, [0])
         nc.sync.dma_start(offs_sb[:], offs)
         load_gate(nc.scalar, 0)
-        load_gate(nc.scalar, 1)
+        load_gate(nc.sync, 1)
         load_planes(0, range(1, PACK))
         load_planes(1, range(PACK))
         load_gate(nc.sync, 2)

@@ -9,21 +9,15 @@ P = 128
 PACK = 4
 PASSES = K // (P * PACK)
 UNIT = 128
+UNITS = S // UNIT
 PER_COLUMN = 16
-
-STEPS = [(0, 5, 0), (0, 5, 1), (0, 8, 2), (5, 3, 0), (5, 5, 1), (8, 2, 0), (8, 1, 2), (9, 1, 2)]
-LAST = len(STEPS) - 1
-FIRST_GROUP, SECOND_GROUP, THIRD_GROUP = range(0, 5), range(5, 8), range(8, 10)
-WIDE_STEPS = (2, 4)
 SPARE = 16
-GATE_CUTS = [0, 192, 640, 1024, S]
-GATE_SHIFT = 32
-OUT_PIECES = [(0, 448), (448, 192)]
 
-SUM_BANK = [0, 1, 2, 3, 4, 4, 6, 3, 0, 1]
-TURN_RUNS = [(0, 2, 5), (2, 2, 6), (4, 2, 7), (6, 2, 5), (8, 1, 2), (9, 1, 4)]
-RESULT_RUNS = [(0, 4, 6), (4, 4, 3), (8, 1, 0), (9, 1, 1)]
-HALVED = (7, 9)
+EARLY = 4
+GATE_CUTS = [0, 192, 512, 896, S]
+SUM_BANK = [0, 1, 2, 3, 4, 5, 6, 7, 1, 2]
+TURN_RUNS = [(0, 2, 0), (2, 2, 3), (4, 2, 4), (6, 2, 5), (8, 1, 6), (9, 1, 7)]
+OUT_PIECES = [(0, 192), (192, 256), (448, 192)]
 
 FLOPS = 2 * S * (K * H + H * N)
 BYTES = 4 * K * T + E * (K * H + H * N) // 2 + E * (K * H + H * N) // 32 + 4 * S + 2 * P * (S + 2 * T) // 16 + 4 * N * T
@@ -39,23 +33,15 @@ FP4X4 = mybir.dt.float4_e2m1fn_x4
 MULT = mybir.AluOpType.mult
 ADD = mybir.AluOpType.add
 SILU = mybir.ActivationFunctionType.Silu
-
-
-def chunks(units, widest):
-    runs, done = [], 0
-    while done < units:
-        size = max(w for w in (8, 4, 2, 1) if w <= min(widest, units - done))
-        runs.append((done, size))
-        done += size
-    return runs
+COPY = mybir.ActivationFunctionType.Copy
 
 
 def slots(first, units):
     return slice(first * UNIT, (first + units) * UNIT)
 
 
-def run_of(runs, u):
-    return [run for run in runs if run[0] <= u][-1]
+def entries(lo, hi):
+    return slice(lo // PER_COLUMN, hi // PER_COLUMN)
 
 
 def tile_moe_pre_mlp_silu_kernel(
@@ -64,20 +50,18 @@ def tile_moe_pre_mlp_silu_kernel(
     nc = tc.nc
     with ExitStack() as ctx:
         held = ctx.enter_context(tc.tile_pool(name="held", bufs=1))
-        ring = ctx.enter_context(tc.tile_pool(name="ring", bufs=2))
         psum = ctx.enter_context(tc.psum_pool(name="psum", bufs=1))
 
         offs_sb = held.tile([P, S // PER_COLUMN], U16, name="offs_sb")
         pos1_sb = held.tile([P, T // PER_COLUMN], U16, name="pos1_sb")
         pos2_sb = held.tile([P, T // PER_COLUMN], U16, name="pos2_sb")
-        width = [SPARE + max(units * UNIT for first, units, s in STEPS if s == a) for a in range(PASSES)]
+        width = [SPARE + S, SPARE + S, SPARE + (UNITS - EARLY) * UNIT]
         plane = {
-            (s, t): held.tile([P, width[s]], F32, name=f"plane_{s}_{t}", align_bytes=256)
+            (s, t): held.tile([P, width[s]], F32, name=f"plane_{s}_{t}", align_bytes=64)
             for s in range(PASSES)
             for t in range(PACK)
         }
-        gate_tile = held.tile([P, GATE_SHIFT + S], F32, name="gate_tile", align_bytes=256)
-        gate_sb = gate_tile[:, GATE_SHIFT:]
+        gate_sb = held.tile([P, S], F32, name="gate_sb", align_bytes=64)
         w1_sb = [held.tile([P, PASSES, 2 * H], U8, name=f"w1_{e}", align_bytes=64) for e in range(E)]
         w2_sb = held.tile([P, E, 2 * N], U8, name="w2_sb", align_bytes=64)
         w1_scale_sb = held.tile([P, E * PASSES, H], U8, name="w1_scale_sb", align_bytes=64)
@@ -85,20 +69,25 @@ def tile_moe_pre_mlp_silu_kernel(
         ident = held.tile([P, P], F32, name="ident")
         y_sb = held.tile([P, S], F32, name="y_sb")
 
-        for t in range(PACK):
-            nc.vector.memset(plane[0, t][:, T:], 0.0)
+        warm = held.tile([P, 2], F32, name="warm")
+        nc.vector.memset(warm[:, 0:1], 0.0)
+        nc.scalar.activation(warm[:, 1:2], warm[:, 0:1], SILU)
+
+        nc.vector.memset(plane[1, 0][:, T:], 0.0)
         nc.vector.memset(w1_scale_sb[:].rearrange("p a i -> p (a i)").bitcast(I32), 0)
         nc.vector.memset(w2_scale_sb[:].rearrange("p a i -> p (a i)").bitcast(I32), 0)
+        for t in range(PACK):
+            for s in range(2):
+                if (s, t) != (1, 0):
+                    nc.gpsimd.memset(plane[s, t][:, T:], 0.0)
+        for t in range(PACK):
+            nc.gpsimd.memset(plane[2, t][:, T:], 0.0)
         make_identity(nc, ident[:])
-        for s in range(1, PASSES):
-            for t in range(PACK):
-                nc.gpsimd.memset(plane[s, t][:, T:], 0.0)
 
         x_rows = xT.rearrange("(s p t) c -> s t p c", p=P, t=PACK)
 
-        def load_planes(s, rows):
-            for t in rows:
-                nc.sync.dma_start(plane[s, t][:, 0:T], x_rows[s, t])
+        def load_plane(s, t):
+            nc.sync.dma_start(plane[s, t][:, 0:T], x_rows[s, t])
 
         def load_gate(queue, piece):
             cols = slice(GATE_CUTS[piece], GATE_CUTS[piece + 1])
@@ -109,15 +98,18 @@ def tile_moe_pre_mlp_silu_kernel(
             for quad in range(4):
                 nc.sync.dma_start(scale_sb[32 * quad : 32 * quad + 4].bitcast(I32), rows[4 * quad : 4 * quad + 4])
 
-        load_planes(0, [0])
+        load_plane(1, 0)
         nc.sync.dma_start(offs_sb[:], offs)
-        load_gate(nc.scalar, 0)
+        load_plane(0, 0)
+        load_gate(nc.sync, 0)
         load_gate(nc.sync, 1)
-        load_planes(0, range(1, PACK))
-        load_planes(1, range(PACK))
         load_gate(nc.sync, 2)
-        load_planes(2, range(PACK))
         load_gate(nc.sync, 3)
+        for t in range(1, PACK):
+            load_plane(0, t)
+            load_plane(1, t)
+        for t in range(PACK):
+            load_plane(2, t)
         load_scales(w1_scale_sb, w1_scales)
         load_scales(w2_scale_sb, w2_scales)
         for e in range(E):
@@ -126,193 +118,197 @@ def tile_moe_pre_mlp_silu_kernel(
         nc.sync.dma_start(pos1_sb[:], pos1)
         nc.sync.dma_start(pos2_sb[:], pos2)
 
-        picked, rounded, x_codes, x_scales = {}, {}, {}, {}
-        sums, passes_done, waiting, hidden = {}, {}, {}, {}
-        turned, h_rounded, results = {}, {}, {}
+        runs = [(0, 0, UNITS), (1, 0, UNITS), (2, 0, EARLY), (2, EARLY, UNITS - EARLY)]
+        picked = {
+            (s, first): held.tile([P, PACK, units * UNIT], F32, name=f"picked_{s}_{first}", align_bytes=64)
+            for s, first, units in runs
+        }
         h_codes = held.tile([P, S], U32, name="h_codes", align_bytes=64)
+        h_scales = held.tile([P, S], U8, name="h_scales", align_bytes=64)
+        h_rounded = {
+            first: held.tile([P, units * UNIT * PACK], BF16, name=f"h_rounded_{first}", align_bytes=64)
+            for first, units in [(0, 4), (4, 4), (8, 2)]
+        }
+        operand, sums, hidden, turned, results = {}, {}, {}, {}, {}
 
-        def gather(k):
-            first, units, s = STEPS[k]
-            lo, hi = first * UNIT, (first + units) * UNIT
-            picked[k] = ring.tile([P, PACK, hi - lo], F32, name=f"picked_{k}", tag="picked", align_bytes=256)
-            for t in range(PACK):
-                ends = GATE_CUTS[:3] if (k, t) == (0, 0) else [lo, hi]
-                for a, b in zip(ends, ends[1:]):
-                    tokens = plane[s, t][:].indirect(offs_sb[:, a // PER_COLUMN : b // PER_COLUMN])
-                    nc.vector.tensor_tensor(picked[k][:, t, a - lo : b - lo], tokens, gate_sb[:, a:b], MULT)
-                if t == 0 and k - 2 in WIDE_STEPS:
-                    first_layer(k - 2, slice(1, None))
+        def planes_of(s, cols):
+            first = max(f for a, f in picked if a == s and f * UNIT <= cols.start)
+            return picked[s, first][:, :, cols.start - first * UNIT : cols.stop - first * UNIT]
 
-        def round_rows(k, into, runs):
-            rounded[k] = into
-            for a, units in runs:
-                nc.scalar.copy(
-                    into[:, slots(a, units), :].rearrange("p (c i) t -> p c t i", i=4),
-                    picked[k][:, :, slots(a, units)].rearrange("p t (c i) -> p c t i", i=4),
-                )
+        def gather_gated(t, lo, hi):
+            tokens = plane[0, t][:].indirect(offs_sb[:, entries(lo, hi)])
+            nc.vector.tensor_tensor(planes_of(0, slice(lo, hi))[:, t, :], tokens, gate_sb[:, lo:hi], MULT)
 
-        def round_step(k, tag):
-            units = STEPS[k][1]
-            into = held.tile([P, units * UNIT, PACK], BF16, name=f"rounded_{k}", tag=tag, align_bytes=64)
-            round_rows(k, into, chunks(units, 4))
+        def gather_plain(s, t, first, units):
+            cols = slots(first, units)
+            tokens = plane[s, t][:].indirect(offs_sb[:, entries(cols.start, cols.stop)])
+            nc.scalar.activation(planes_of(s, cols)[:, t, :], tokens, COPY)
 
-        def multiply(u, s, codes, scales):
-            e, done = u * UNIT // C, passes_done.get(u, 0)
-            if done == 0:
+        def batch(name, blocks):
+            total = sum(units for s, first, units in blocks)
+            values = held.tile([P, total * UNIT, PACK], BF16, name=f"rounded_{name}", align_bytes=64)
+            places, done = {}, 0
+            for s, first, units in blocks:
+                places[s, first, units] = slots(done, units)
+                done += units
+            return name, values, places
+
+        def round_into(into, s, first, units):
+            name, values, places = into
+            cols = slots(first, units)
+            rows = values[:, places[s, first, units], :].rearrange("p (c i) t -> p c t i", i=4)
+            planes = planes_of(s, cols).rearrange("p t (c i) -> p c t i", i=4)
+            if s == 0:
+                nc.vector.tensor_copy(rows, planes)
+            else:
+                weights = gate_sb[:, cols].rearrange("p (c i) -> p c i", i=4).unsqueeze(2)
+                nc.vector.tensor_tensor(rows, planes, weights.to_broadcast([P, units * UNIT // 4, PACK, 4]), MULT)
+
+        def quantise(into):
+            name, values, places = into
+            count = values.shape[1]
+            codes = held.tile([P, count], U32, name=f"x_codes_{name}", align_bytes=64)
+            scales = held.tile([P, count], U8, name=f"x_scales_{name}", align_bytes=64)
+            nc.vector.quantize_mx(codes[:].bitcast(FP8X4), scales[:], values[:].rearrange("p c t -> p (c t)"))
+            for (s, first, units), place in places.items():
+                for b in range(units):
+                    cols = slice(place.start + b * UNIT, place.start + (b + 1) * UNIT)
+                    operand[first + b, s] = codes[:, cols], scales[:, cols]
+
+        def multiply(u, s):
+            e = u * UNIT // C
+            if s == 0:
                 sums[u] = psum.tile([P, H], F32, name=f"sums_{u}", tag=f"bank_{SUM_BANK[u]}")
+            codes, scales = operand[u, s]
             nc.tensor.matmul_mx(
                 out=sums[u][:],
                 lhsT=codes.bitcast(FP8X4),
                 lhsT_scale=scales,
                 rhs=w1_sb[e][:, s, :].bitcast(FP4X4),
                 rhs_scale=w1_scale_sb[:, e * PASSES + s, :],
-                start=(done == 0),
-                stop=(done == PASSES - 1),
+                start=(s == 0),
+                stop=(s == PASSES - 1),
             )
-            passes_done[u] = done + 1
 
-        def quantise(codes, scales, values):
-            nc.vector.quantize_mx(codes.bitcast(FP8X4), scales, values.rearrange("p c t -> p (c t)"))
+        def finish(units):
+            for u in units:
+                multiply(u, 1)
+                multiply(u, 2)
 
-        def first_layer_of_two_steps(values):
-            count = 2 * len(FIRST_GROUP)
-            codes = held.tile([P, count * UNIT], U32, name="x_codes_first", align_bytes=64)
-            scales = held.tile([P, count * UNIT], U8, name="x_scales_first", align_bytes=64)
-            for a, units in chunks(count, 8):
-                quantise(codes[:, slots(a, units)], scales[:, slots(a, units)], values[:, slots(a, units), :])
-                for b in range(a, a + units):
-                    k, u = divmod(b, len(FIRST_GROUP))
-                    multiply(u, STEPS[k][2], codes[:, slots(b, 1)], scales[:, slots(b, 1)])
-
-        def first_layer(k, parts):
-            first, units, s = STEPS[k]
-            if k not in x_codes:
-                x_codes[k] = held.tile([P, units * UNIT], U32, name=f"x_codes_{k}", align_bytes=64)[:]
-            if k not in x_scales:
-                x_scales[k] = held.tile([P, units * UNIT], U8, name=f"x_scales_{k}", align_bytes=64)
-            for a, size in chunks(units, 4)[parts]:
-                quantise(x_codes[k][:, slots(a, size)], x_scales[k][:, slots(a, size)], rounded[k][:, slots(a, size), :])
-                for b in range(a, a + size):
-                    u = first + b
-                    waiting.setdefault(u, []).append((s, x_codes[k][:, slots(b, 1)], x_scales[k][:, slots(b, 1)]))
-                    if u not in SECOND_GROUP or len(waiting[u]) + passes_done.get(u, 0) > 1:
-                        for queued in waiting.pop(u):
-                            multiply(u, *queued)
-
-        def first_layer_behind(k):
-            first_layer(k - 1, slice(0, 1) if k - 1 in WIDE_STEPS else slice(None))
-
-        def silu(u):
-            by_half = sums[u][:].rearrange("c (p v d) -> c v p d", v=2, d=2)
-            if u in HALVED:
-                hidden[u] = [held.tile([P, P, 2], BF16, name=f"hidden_{u}_{v}", align_bytes=64)[:] for v in range(2)]
-                for v in range(2):
-                    nc.scalar.activation(hidden[u][v], by_half[:, v], SILU)
-            else:
-                whole = held.tile([P, 2, P, 2], BF16, name=f"hidden_{u}", align_bytes=64)
-                nc.scalar.activation(whole[:], by_half, SILU)
-                hidden[u] = [whole[:, v] for v in range(2)]
+        def silu(units):
+            for u in units:
+                by_half = sums[u][:].rearrange("c (p v d) -> c v p d", v=2, d=2)
+                hidden[u] = held.tile([P, 2, P, 2], BF16, name=f"hidden_{u}", align_bytes=64)
+                nc.scalar.activation(hidden[u][:], by_half, SILU)
 
         def turn(u):
-            first, units, bank = run_of(TURN_RUNS, u)
+            first, units, bank = [run for run in TURN_RUNS if run[0] <= u][-1]
             if u == first:
                 turned[first] = psum.tile([P, units, 2, UNIT], F32, name=f"turned_{first}", tag=f"bank_{bank}")
             for v in range(2):
-                pairs = hidden[u][v].rearrange("c p d -> c (p d)").bitcast(F32)
+                pairs = hidden[u][:, v].rearrange("c p d -> c (p d)").bitcast(F32)
                 nc.tensor.transpose(turned[first][:, u - first, v, :], pairs, ident[:])
 
-        def h_rows(u, units):
-            first, count, tag = run_of([(0, 4, "h_rounded_0"), (4, 4, f"rounded_{LAST}"), (8, 2, "h_rounded_8")], u)
-            if first not in h_rounded:
-                h_rounded[first] = held.tile([P, count * UNIT * PACK], BF16, name=f"h_rounded_{first}", tag=tag, align_bytes=64)
-            return h_rounded[first][:, (u - first) * UNIT * PACK : (u - first + units) * UNIT * PACK]
+        def h_rows(first, units):
+            base = max(f for f in h_rounded if f <= first)
+            return h_rounded[base][:, (first - base) * UNIT * PACK : (first - base + units) * UNIT * PACK]
 
         def weave(first, copy):
-            units = run_of(TURN_RUNS, first)[1]
+            units = turned[first].shape[1]
             words = h_rows(first, units).bitcast(F32).rearrange("p (u c v) -> p u c v", u=units, v=2)
             copy(words, turned[first][:].rearrange("p u v c -> p u c v"))
 
-        def second_layer(u, units, h_scales):
-            cols = slots(u, units)
-            nc.vector.quantize_mx(h_codes[:, cols].bitcast(FP8X4), h_scales[:, cols], h_rows(u, units))
-            first, count, bank = run_of(RESULT_RUNS, u)
-            if u == first:
-                results[first] = psum.tile([P, count * UNIT], F32, name=f"results_{first}", tag=f"bank_{bank}")
+        def second_layer(first, units, bank):
+            cols = slots(first, units)
+            nc.vector.quantize_mx(h_codes[:, cols].bitcast(FP8X4), h_scales[:, cols], h_rows(first, units))
+            results[first] = psum.tile([P, units * UNIT], F32, name=f"results_{first}", tag=f"bank_{bank}")
             for a in range(cols.start, cols.stop, C):
-                b = min(a + C, cols.stop)
                 nc.tensor.matmul_mx(
-                    out=results[first][:, a - first * UNIT : b - first * UNIT],
+                    out=results[first][:, a - cols.start : a - cols.start + C],
                     lhsT=w2_sb[:, a // C, :].bitcast(FP4X4),
                     lhsT_scale=w2_scale_sb[:, a // C, :],
-                    rhs=h_codes[:, a:b].bitcast(FP8X4),
-                    rhs_scale=h_scales[:, a:b],
+                    rhs=h_codes[:, a : a + C].bitcast(FP8X4),
+                    rhs_scale=h_scales[:, a : a + C],
                     start=True,
                     stop=True,
                 )
 
-        group_units = len(FIRST_GROUP)
-        gather(0)
-        two_steps = held.tile([P, 2 * group_units * UNIT, PACK], BF16, name="two_steps", align_bytes=64)
-        round_rows(0, two_steps[:, slots(0, group_units), :], [(0, group_units)])
-        gather(1)
-        round_rows(1, two_steps[:, slots(group_units, group_units), :], [(0, group_units)])
-        gather(2)
-        first_layer_of_two_steps(two_steps)
-        round_step(2, "rounded_2")
-        gather(3)
-        first_layer_behind(3)
-        round_step(3, "rounded_3")
+        for t in range(PACK):
+            ends = GATE_CUTS if t == 0 else [0, S]
+            for lo, hi in zip(ends, ends[1:]):
+                gather_gated(t, lo, hi)
+            gather_plain(1, t, 0, UNITS)
+        for first, units in [(0, EARLY), (EARLY, UNITS - EARLY)]:
+            for t in range(PACK):
+                gather_plain(2, t, first, units)
 
-        gather(4)
-        for u in FIRST_GROUP:
-            silu(u)
-            turn(u)
-            if u % 2 == 1:
-                weave(u - 1, nc.scalar.copy)
-        first_layer_behind(4)
-        round_step(4, "hidden_3")
-        gather(5)
-        first_layer_behind(5)
-        round_step(5, "hidden_4")
+        blocks = [(0, 0, 8), (0, 8, 2), (1, 0, 4), (2, 0, 2), (2, 2, 2), (1, 4, 2), (2, 4, 2), (1, 6, 2), (2, 6, 2)]
+        blocks = blocks + [(1, 8, 2), (2, 8, 1), (2, 9, 1)]
+        values = {block: batch(f"{block[0]}_{block[1]}", [block]) for block in blocks}
 
-        for u in SECOND_GROUP:
-            silu(u)
-            turn(u)
-        gather(6)
-        first_layer_behind(6)
-        round_step(6, "hidden_5")
-        gather(LAST)
+        def step(block, before):
+            round_into(values[block], *block)
+            quantise(values[before])
 
-        last_codes = held.tile([P, 2 * UNIT], U32, name="last_codes", tag="hidden_7_0", align_bytes=64)
-        x_codes[LAST - 1], x_codes[LAST] = last_codes[:, slots(0, 1)], last_codes[:, slots(1, 1)]
-        first_layer_behind(LAST)
-        round_step(LAST, f"rounded_{LAST}")
+        def passes(s, units):
+            for u in units:
+                multiply(u, s)
 
-        early_scales = held.tile([P, S], U8, name="early_scales", tag="hidden_7_1", align_bytes=64)
-        second_layer(0, 2, early_scales)
-        first_layer(LAST, slice(None))
-        for u in THIRD_GROUP:
-            silu(u)
-        for u in THIRD_GROUP:
-            turn(u)
-            weave(u, nc.scalar.copy)
-        late_scales = held.tile([P, S], U8, name="late_scales", tag=f"x_scales_{LAST}", align_bytes=64)
-        for first in (4, 6):
-            weave(first, nc.vector.tensor_copy)
-        for u, units in [(2, 2), (4, 4), (8, 1), (9, 1)]:
-            second_layer(u, units, late_scales)
+        round_into(values[0, 0, 8], 0, 0, 8)
+        step((0, 8, 2), (0, 0, 8))
+        passes(0, range(8))
+        step((1, 0, 4), (0, 8, 2))
+        step((2, 0, 2), (1, 0, 4))
+        passes(1, range(4))
+        step((2, 2, 2), (2, 0, 2))
+        passes(2, range(2))
+        step((1, 4, 2), (2, 2, 2))
+        passes(2, range(2, 4))
+        silu(range(4))
+        step((2, 4, 2), (1, 4, 2))
+        passes(1, range(4, 6))
+        turn(0)
+        turn(1)
+        weave(0, nc.scalar.copy)
+        multiply(8, 0)
+        step((1, 6, 2), (2, 4, 2))
+        passes(2, range(4, 6))
+        silu(range(4, 6))
+        multiply(9, 0)
+        turn(2)
+        turn(3)
+        weave(2, nc.scalar.copy)
+        step((2, 6, 2), (1, 6, 2))
+        passes(1, range(6, 8))
+        turn(4)
+        turn(5)
+        weave(4, nc.scalar.copy)
+        step((1, 8, 2), (2, 6, 2))
+        passes(2, range(6, 8))
+        silu(range(6, 8))
+        step((2, 8, 1), (1, 8, 2))
+        passes(1, range(8, 10))
+        step((2, 9, 1), (2, 8, 1))
+        quantise(values[2, 9, 1])
+        turn(6)
+        passes(2, range(8, 10))
+        silu(range(8, 10))
+        turn(7)
+        second_layer(0, 4, 0)
+        weave(6, nc.vector.tensor_copy)
+        turn(8)
+        weave(8, nc.vector.tensor_copy)
+        turn(9)
+        weave(9, nc.scalar.copy)
+        second_layer(4, 4, 3)
+        second_layer(8, 2, 4)
+        nc.scalar.copy(y_sb[:, slots(0, 4)], results[0][:])
+        nc.scalar.copy(y_sb[:, slots(4, 4)], results[4][:])
+        nc.vector.tensor_copy(y_sb[:, slots(8, 2)], results[8][:])
 
-        for first, units, bank in RESULT_RUNS:
-            copy = nc.vector.tensor_copy if first == RESULT_RUNS[1][0] else nc.scalar.copy
-            copy(y_sb[:, slots(first, units)], results[first][:])
-
-        by_pos1 = []
         for lo, n in OUT_PIECES:
             one = held.tile([P, n], F32, name=f"one_{lo}")
-            nc.vector.tensor_copy(one[:], y_sb[:].indirect(pos1_sb[:, lo // PER_COLUMN : (lo + n) // PER_COLUMN]))
-            by_pos1.append(one)
-        for (lo, n), one in zip(OUT_PIECES, by_pos1):
+            nc.scalar.activation(one[:], y_sb[:].indirect(pos1_sb[:, entries(lo, lo + n)]), COPY)
             both = held.tile([P, n], F32, name=f"both_{lo}")
-            other = y_sb[:].indirect(pos2_sb[:, lo // PER_COLUMN : (lo + n) // PER_COLUMN])
-            nc.vector.tensor_tensor(both[:], other, one[:], ADD)
+            nc.vector.tensor_tensor(both[:], y_sb[:].indirect(pos2_sb[:, entries(lo, lo + n)]), one[:], ADD)
             nc.sync.dma_start(out[:, lo : lo + n], both[:])

@@ -156,13 +156,14 @@ def tile_moe_pre_mlp_silu_kernel(
         def round_into(into, s, first, units):
             name, values, places = into
             cols = slots(first, units)
-            rows = values[:, places[s, first, units], :].rearrange("p (c i) t -> p c t i", i=4)
-            planes = planes_of(s, cols).rearrange("p t (c i) -> p c t i", i=4)
+            run = 4 if s == 0 else 2
+            rows = values[:, places[s, first, units], :].rearrange("p (c i) t -> p c t i", i=run)
+            planes = planes_of(s, cols).rearrange("p t (c i) -> p c t i", i=run)
             if s == 0:
                 nc.vector.tensor_copy(rows, planes)
             else:
-                weights = gate_sb[:, cols].rearrange("p (c i) -> p c i", i=4).unsqueeze(2)
-                nc.vector.tensor_tensor(rows, planes, weights.to_broadcast([P, units * UNIT // 4, PACK, 4]), MULT)
+                weights = gate_sb[:, cols].rearrange("p (c i) -> p c i", i=run).unsqueeze(2)
+                nc.vector.tensor_tensor(rows, planes, weights.to_broadcast([P, units * UNIT // run, PACK, run]), MULT)
 
         def quantise(into):
             name, values, places = into

@@ -69,10 +69,6 @@ def tile_moe_pre_mlp_silu_kernel(
         ident = held.tile([P, P], F32, name="ident")
         y_sb = held.tile([P, S], F32, name="y_sb")
 
-        warm = held.tile([P, 2], F32, name="warm")
-        nc.vector.memset(warm[:, 0:1], 0.0)
-        nc.scalar.activation(warm[:, 1:2], warm[:, 0:1], SILU)
-
         nc.vector.memset(plane[1, 0][:, T:], 0.0)
         nc.vector.memset(w1_scale_sb[:].rearrange("p a i -> p (a i)").bitcast(I32), 0)
         nc.vector.memset(w2_scale_sb[:].rearrange("p a i -> p (a i)").bitcast(I32), 0)

@@ -13,10 +13,10 @@ UNITS = S // UNIT
 PER_COLUMN = 16
 SPARE = 16
 
-EARLY = 4
-GATE_CUTS = [0, 192, 512, 896, S]
-SUM_BANK = [0, 1, 2, 3, 4, 5, 6, 7, 1, 2]
-TURN_RUNS = [(0, 2, 0), (2, 2, 3), (4, 2, 4), (6, 2, 5), (8, 1, 6), (9, 1, 7)]
+GATED = 10
+GATE_CUTS = [0, 192, 512, 1024, S]
+SUM_BANK = [0, 1, 2, 3, 4, 5, 6, 7, 0, 1]
+REUSE = {(0, 8): "rounded_2_0", (1, 4): "picked_2_0", (2, 4): "rounded_2_1", (1, 6): "rounded_2_2", (1, 8): "rounded_1_4"}
 OUT_PIECES = [(0, 192), (192, 256), (448, 192)]
 
 FLOPS = 2 * S * (K * H + H * N)
@@ -55,7 +55,7 @@ def tile_moe_pre_mlp_silu_kernel(
         offs_sb = held.tile([P, S // PER_COLUMN], U16, name="offs_sb")
         pos1_sb = held.tile([P, T // PER_COLUMN], U16, name="pos1_sb")
         pos2_sb = held.tile([P, T // PER_COLUMN], U16, name="pos2_sb")
-        width = [SPARE + S, SPARE + S, SPARE + (UNITS - EARLY) * UNIT]
+        width = [T, SPARE + S, T]
         plane = {
             (s, t): held.tile([P, width[s]], F32, name=f"plane_{s}_{t}", align_bytes=64)
             for s in range(PASSES)
@@ -69,15 +69,13 @@ def tile_moe_pre_mlp_silu_kernel(
         ident = held.tile([P, P], F32, name="ident")
         y_sb = held.tile([P, S], F32, name="y_sb")
 
-        nc.vector.memset(plane[1, 0][:, T:], 0.0)
+        warm = held.tile([P, 2], F32, name="warm")
+        nc.vector.memset(warm[:, 0:1], 0.0)
+        nc.scalar.activation(warm[:, 1:2], warm[:, 0:1], SILU)
         nc.vector.memset(w1_scale_sb[:].rearrange("p a i -> p (a i)").bitcast(I32), 0)
         nc.vector.memset(w2_scale_sb[:].rearrange("p a i -> p (a i)").bitcast(I32), 0)
         for t in range(PACK):
-            for s in range(2):
-                if (s, t) != (1, 0):
-                    nc.gpsimd.memset(plane[s, t][:, T:], 0.0)
-        for t in range(PACK):
-            nc.gpsimd.memset(plane[2, t][:, T:], 0.0)
+            nc.gpsimd.memset(plane[1, t][:, T:], 0.0)
         make_identity(nc, ident[:])
 
         x_rows = xT.rearrange("(s p t) c -> s t p c", p=P, t=PACK)
@@ -85,47 +83,44 @@ def tile_moe_pre_mlp_silu_kernel(
         def load_plane(s, t):
             nc.sync.dma_start(plane[s, t][:, 0:T], x_rows[s, t])
 
-        def load_gate(queue, piece):
+        def load_gate(piece):
             cols = slice(GATE_CUTS[piece], GATE_CUTS[piece + 1])
-            queue.dma_start(gate_sb[:, cols], gate[0:P, cols])
+            nc.sync.dma_start(gate_sb[:, cols], gate[0:P, cols])
 
         def load_scales(scale_sb, scales):
-            rows = scales.rearrange("e s q i -> q (e s) i").bitcast(I32)
-            for quad in range(4):
-                nc.sync.dma_start(scale_sb[32 * quad : 32 * quad + 4].bitcast(I32), rows[4 * quad : 4 * quad + 4])
+            rows = scales.rearrange("e s (q r) i -> r q (e s) i", r=4).bitcast(I32)
+            for r in range(4):
+                nc.sync.dma_start(scale_sb[r:P:32].bitcast(I32), rows[r])
+
+        def load_w1(e):
+            nc.sync.dma_start(w1_sb[e][:].bitcast(I32), w1_words[e].rearrange("s p b -> p s b").bitcast(I32))
 
         load_plane(1, 0)
         nc.sync.dma_start(offs_sb[:], offs)
         load_plane(0, 0)
-        load_gate(nc.sync, 0)
-        load_gate(nc.sync, 1)
-        load_gate(nc.sync, 2)
-        load_gate(nc.sync, 3)
+        for piece in range(4):
+            load_gate(piece)
         for t in range(1, PACK):
             load_plane(0, t)
             load_plane(1, t)
         for t in range(PACK):
             load_plane(2, t)
         load_scales(w1_scale_sb, w1_scales)
-        load_scales(w2_scale_sb, w2_scales)
         for e in range(E):
-            nc.sync.dma_start(w1_sb[e][:].bitcast(I32), w1_words[e].rearrange("s p b -> p s b").bitcast(I32))
+            load_w1(e)
         nc.sync.dma_start(w2_sb[:].bitcast(I32), w2_words.rearrange("e s p b -> p (e s) b").bitcast(I32))
+        load_scales(w2_scale_sb, w2_scales)
         nc.sync.dma_start(pos1_sb[:], pos1)
         nc.sync.dma_start(pos2_sb[:], pos2)
 
-        runs = [(0, 0, UNITS), (1, 0, UNITS), (2, 0, EARLY), (2, EARLY, UNITS - EARLY)]
-        picked = {
-            (s, first): held.tile([P, PACK, units * UNIT], F32, name=f"picked_{s}_{first}", align_bytes=64)
-            for s, first, units in runs
-        }
         h_codes = held.tile([P, S], U32, name="h_codes", align_bytes=64)
         h_scales = held.tile([P, S], U8, name="h_scales", align_bytes=64)
-        h_rounded = {
-            first: held.tile([P, units * UNIT * PACK], BF16, name=f"h_rounded_{first}", align_bytes=64)
-            for first, units in [(0, 4), (4, 4), (8, 2)]
-        }
-        operand, sums, hidden, turned, results = {}, {}, {}, {}, {}
+        picked, values, operand, sums, hidden, turned, h_rounded, results = {}, {}, {}, {}, {}, {}, {}, {}
+
+        def run(s, first, units, tag=""):
+            picked[s, first] = held.tile(
+                [P, PACK, units * UNIT], F32, name=f"picked_{s}_{first}", tag=tag, align_bytes=64
+            )
 
         def planes_of(s, cols):
             first = max(f for a, f in picked if a == s and f * UNIT <= cols.start)
@@ -140,71 +135,72 @@ def tile_moe_pre_mlp_silu_kernel(
             tokens = plane[s, t][:].indirect(offs_sb[:, entries(cols.start, cols.stop)])
             nc.scalar.activation(planes_of(s, cols)[:, t, :], tokens, COPY)
 
-        def batch(name, blocks):
-            total = sum(units for s, first, units in blocks)
-            values = held.tile([P, total * UNIT, PACK], BF16, name=f"rounded_{name}", align_bytes=64)
-            places, done = {}, 0
-            for s, first, units in blocks:
-                places[s, first, units] = slots(done, units)
-                done += units
-            return name, values, places
+        def gather_run(s, first, units, tag=""):
+            run(s, first, units, tag)
+            for t in range(PACK):
+                gather_plain(s, t, first, units)
 
-        def round_into(into, s, first, units):
-            name, values, places = into
+        def round_block(s, first, units):
+            values[s, first] = held.tile(
+                [P, units * UNIT, PACK], BF16, name=f"rounded_{s}_{first}", tag=REUSE.get((s, first), ""), align_bytes=64
+            )
             cols = slots(first, units)
-            run = 4 if s == 0 else 2
-            rows = values[:, places[s, first, units], :].rearrange("p (c i) t -> p c t i", i=run)
-            planes = planes_of(s, cols).rearrange("p t (c i) -> p c t i", i=run)
-            if s == 0:
+            gated = s == 0 and first < GATED
+            near = 4 if gated else 2
+            rows = values[s, first][:].rearrange("p (c i) t -> p c t i", i=near)
+            planes = planes_of(s, cols).rearrange("p t (c i) -> p c t i", i=near)
+            if gated:
                 nc.vector.tensor_copy(rows, planes)
             else:
-                weights = gate_sb[:, cols].rearrange("p (c i) -> p c i", i=run).unsqueeze(2)
-                nc.vector.tensor_tensor(rows, planes, weights.to_broadcast([P, units * UNIT // run, PACK, run]), MULT)
+                weights = gate_sb[:, cols].rearrange("p (c i) -> p c i", i=near).unsqueeze(2)
+                nc.vector.tensor_tensor(rows, planes, weights.to_broadcast([P, units * UNIT // near, PACK, near]), MULT)
 
-        def quantise(into):
-            name, values, places = into
-            count = values.shape[1]
-            codes = held.tile([P, count], U32, name=f"x_codes_{name}", align_bytes=64)
-            scales = held.tile([P, count], U8, name=f"x_scales_{name}", align_bytes=64)
-            nc.vector.quantize_mx(codes[:].bitcast(FP8X4), scales[:], values[:].rearrange("p c t -> p (c t)"))
-            for (s, first, units), place in places.items():
-                for b in range(units):
-                    cols = slice(place.start + b * UNIT, place.start + (b + 1) * UNIT)
-                    operand[first + b, s] = codes[:, cols], scales[:, cols]
-
-        def multiply(u, s):
-            e = u * UNIT // C
-            if s == 0:
-                sums[u] = psum.tile([P, H], F32, name=f"sums_{u}", tag=f"bank_{SUM_BANK[u]}")
-            codes, scales = operand[u, s]
-            nc.tensor.matmul_mx(
-                out=sums[u][:],
-                lhsT=codes.bitcast(FP8X4),
-                lhsT_scale=scales,
-                rhs=w1_sb[e][:, s, :].bitcast(FP4X4),
-                rhs_scale=w1_scale_sb[:, e * PASSES + s, :],
-                start=(s == 0),
-                stop=(s == PASSES - 1),
+        def quantise(s, first, units):
+            count = units * UNIT
+            codes = held.tile([P, count], U32, name=f"x_codes_{s}_{first}", align_bytes=64)
+            scales = held.tile([P, count], U8, name=f"x_scales_{s}_{first}", align_bytes=64)
+            nc.vector.quantize_mx(
+                codes[:].bitcast(FP8X4), scales[:], values[s, first][:].rearrange("p c t -> p (c t)")
             )
+            for b in range(units):
+                operand[first + b, s] = codes[:, slots(b, 1)], scales[:, slots(b, 1)]
 
-        def finish(units):
-            for u in units:
-                multiply(u, 1)
-                multiply(u, 2)
+        def passes(s, first, units):
+            for u in range(first, first + units):
+                e = u * UNIT // C
+                if s == 0:
+                    sums[u] = psum.tile([P, H], F32, name=f"sums_{u}", tag=f"bank_{SUM_BANK[u]}")
+                codes, scales = operand[u, s]
+                nc.tensor.matmul_mx(
+                    out=sums[u][:],
+                    lhsT=codes.bitcast(FP8X4),
+                    lhsT_scale=scales,
+                    rhs=w1_sb[e][:, s, :].bitcast(FP4X4),
+                    rhs_scale=w1_scale_sb[:, e * PASSES + s, :],
+                    start=(s == 0),
+                    stop=(s == PASSES - 1),
+                )
 
-        def silu(units):
-            for u in units:
+        def step(block, before):
+            round_block(*block)
+            quantise(*before)
+            passes(*before)
+
+        def silu(first, units):
+            for u in range(first, first + units):
                 by_half = sums[u][:].rearrange("c (p v d) -> c v p d", v=2, d=2)
                 hidden[u] = held.tile([P, 2, P, 2], BF16, name=f"hidden_{u}", align_bytes=64)
                 nc.scalar.activation(hidden[u][:], by_half, SILU)
 
-        def turn(u):
-            first, units, bank = [run for run in TURN_RUNS if run[0] <= u][-1]
-            if u == first:
-                turned[first] = psum.tile([P, units, 2, UNIT], F32, name=f"turned_{first}", tag=f"bank_{bank}")
-            for v in range(2):
-                pairs = hidden[u][:, v].rearrange("c p d -> c (p d)").bitcast(F32)
-                nc.tensor.transpose(turned[first][:, u - first, v, :], pairs, ident[:])
+        def turn(first, units, bank):
+            turned[first] = psum.tile([P, units, 2, UNIT], F32, name=f"turned_{first}", tag=f"bank_{bank}")
+            for u in range(first, first + units):
+                for v in range(2):
+                    pairs = hidden[u][:, v].rearrange("c p d -> c (p d)").bitcast(F32)
+                    nc.tensor.transpose(turned[first][:, u - first, v, :], pairs, ident[:])
+
+        for first, units in [(0, 4), (4, 4), (8, 2)]:
+            h_rounded[first] = held.tile([P, units * UNIT * PACK], BF16, name=f"h_rounded_{first}", align_bytes=64)
 
         def h_rows(first, units):
             base = max(f for f in h_rounded if f <= first)
@@ -230,74 +226,58 @@ def tile_moe_pre_mlp_silu_kernel(
                     stop=True,
                 )
 
+        run(0, 0, 4)
+        run(0, 4, 4)
+        run(0, 8, 2)
+        run(1, 0, UNITS)
         for t in range(PACK):
-            ends = GATE_CUTS if t == 0 else [0, S]
+            ends = GATE_CUTS if t == 0 else [0, 512, 1024, S]
             for lo, hi in zip(ends, ends[1:]):
                 gather_gated(t, lo, hi)
             gather_plain(1, t, 0, UNITS)
-        for first, units in [(0, EARLY), (EARLY, UNITS - EARLY)]:
-            for t in range(PACK):
-                gather_plain(2, t, first, units)
+        gather_run(2, 0, 4)
 
-        blocks = [(0, 0, 8), (0, 8, 2), (1, 0, 4), (2, 0, 2), (2, 2, 2), (1, 4, 2), (2, 4, 2), (1, 6, 2), (2, 6, 2)]
-        blocks = blocks + [(1, 8, 2), (2, 8, 1), (2, 9, 1)]
-        values = {block: batch(f"{block[0]}_{block[1]}", [block]) for block in blocks}
-
-        def step(block, before):
-            round_into(values[block], *block)
-            quantise(values[before])
-
-        def passes(s, units):
-            for u in units:
-                multiply(u, s)
-
-        round_into(values[0, 0, 8], 0, 0, 8)
-        step((0, 8, 2), (0, 0, 8))
-        passes(0, range(8))
-        step((1, 0, 4), (0, 8, 2))
-        step((2, 0, 2), (1, 0, 4))
-        passes(1, range(4))
-        step((2, 2, 2), (2, 0, 2))
-        passes(2, range(2))
-        step((1, 4, 2), (2, 2, 2))
-        passes(2, range(2, 4))
-        silu(range(4))
+        round_block(0, 0, 4)
+        gather_run(2, 4, 2, "picked_0_0")
+        step((1, 0, 4), (0, 0, 4))
+        step((0, 4, 4), (1, 0, 4))
+        round_block(2, 0, 1)
+        step((2, 1, 1), (2, 0, 1))
+        step((2, 2, 2), (2, 1, 1))
+        silu(0, 2)
+        gather_run(2, 6, 2, "x_codes_2_1")
+        step((0, 8, 2), (2, 2, 2))
+        silu(2, 2)
+        gather_run(2, 8, 2, "x_codes_2_2")
+        step((1, 4, 2), (0, 4, 4))
+        quantise(0, 8, 2)
         step((2, 4, 2), (1, 4, 2))
-        passes(1, range(4, 6))
-        turn(0)
-        turn(1)
-        weave(0, nc.scalar.copy)
-        multiply(8, 0)
         step((1, 6, 2), (2, 4, 2))
-        passes(2, range(4, 6))
-        silu(range(4, 6))
-        multiply(9, 0)
-        turn(2)
-        turn(3)
-        weave(2, nc.scalar.copy)
-        step((2, 6, 2), (1, 6, 2))
-        passes(1, range(6, 8))
-        turn(4)
-        turn(5)
-        weave(4, nc.scalar.copy)
-        step((1, 8, 2), (2, 6, 2))
-        passes(2, range(6, 8))
-        silu(range(6, 8))
-        step((2, 8, 1), (1, 8, 2))
-        passes(1, range(8, 10))
+        passes(0, 8, 2)
+        step((1, 8, 2), (1, 6, 2))
+        turn(0, 2, 2)
+        turn(2, 2, 3)
+        step((2, 6, 2), (1, 8, 2))
+        weave(0, nc.vector.tensor_copy)
+        quantise(2, 6, 2)
+        passes(2, 6, 2)
+        round_block(2, 8, 1)
         step((2, 9, 1), (2, 8, 1))
-        quantise(values[2, 9, 1])
-        turn(6)
-        passes(2, range(8, 10))
-        silu(range(8, 10))
-        turn(7)
-        second_layer(0, 4, 0)
+        silu(4, 4)
+        turn(4, 2, 4)
+        weave(2, nc.vector.tensor_copy)
+        quantise(2, 9, 1)
+        passes(2, 9, 1)
+        silu(8, 2)
+        second_layer(0, 4, 2)
+        turn(6, 2, 6)
+        weave(4, nc.vector.tensor_copy)
         weave(6, nc.vector.tensor_copy)
-        turn(8)
-        weave(8, nc.vector.tensor_copy)
-        turn(9)
-        weave(9, nc.scalar.copy)
+        turn(8, 1, 7)
+        turn(9, 1, 0)
         second_layer(4, 4, 3)
+        weave(8, nc.vector.tensor_copy)
+        weave(9, nc.vector.tensor_copy)
         second_layer(8, 2, 4)
         nc.scalar.copy(y_sb[:, slots(0, 4)], results[0][:])
         nc.scalar.copy(y_sb[:, slots(4, 4)], results[4][:])

@@ -16,8 +16,8 @@ SPARE = 16
 GATED = 10
 GATE_CUTS = [0, 192, 512, 1024, S]
 SUM_BANK = [0, 1, 2, 3, 4, 5, 6, 7, 0, 1]
-REUSE = {(0, 8): "rounded_2_0", (1, 4): "picked_2_0", (2, 4): "rounded_2_1", (1, 6): "rounded_2_2", (1, 8): "rounded_1_4"}
-OUT_PIECES = [(0, 192), (192, 256), (448, 192)]
+REUSE = {(0, 8): "rounded_2_0", (1, 4): "picked_2_0", (2, 4): "rounded_1_0", (1, 6): "rounded_2_2", (1, 8): "rounded_1_4"}
+OUT_PIECES = [(0, 128), (128, 320), (448, 192)]
 
 FLOPS = 2 * S * (K * H + H * N)
 BYTES = 4 * K * T + E * (K * H + H * N) // 2 + E * (K * H + H * N) // 32 + 4 * S + 2 * P * (S + 2 * T) // 16 + 4 * N * T
@@ -113,7 +113,6 @@ def tile_moe_pre_mlp_silu_kernel(
         nc.sync.dma_start(pos1_sb[:], pos1)
         nc.sync.dma_start(pos2_sb[:], pos2)
 
-        h_codes = held.tile([P, S], U32, name="h_codes", align_bytes=64)
         h_scales = held.tile([P, S], U8, name="h_scales", align_bytes=64)
         picked, values, operand, sums, hidden, turned, h_rounded, results = {}, {}, {}, {}, {}, {}, {}, {}
 
@@ -199,7 +198,7 @@ def tile_moe_pre_mlp_silu_kernel(
                     pairs = hidden[u][:, v].rearrange("c p d -> c (p d)").bitcast(F32)
                     nc.tensor.transpose(turned[first][:, u - first, v, :], pairs, ident[:])
 
-        for first, units in [(0, 4), (4, 4), (8, 2)]:
+        for first, units in [(0, 4), (8, 2)]:
             h_rounded[first] = held.tile([P, units * UNIT * PACK], BF16, name=f"h_rounded_{first}", align_bytes=64)
 
         def h_rows(first, units):
@@ -240,44 +239,42 @@ def tile_moe_pre_mlp_silu_kernel(
         round_block(0, 0, 4)
         gather_run(2, 4, 2, "picked_0_0")
         step((1, 0, 4), (0, 0, 4))
+        gather_run(2, 6, 2, "rounded_0_0")
         step((0, 4, 4), (1, 0, 4))
-        round_block(2, 0, 1)
-        step((2, 1, 1), (2, 0, 1))
-        step((2, 2, 2), (2, 1, 1))
-        silu(0, 2)
-        gather_run(2, 6, 2, "x_codes_2_1")
+        round_block(2, 0, 2)
+        step((2, 2, 2), (2, 0, 2))
         step((0, 8, 2), (2, 2, 2))
-        silu(2, 2)
+        silu(0, 4)
         gather_run(2, 8, 2, "x_codes_2_2")
         step((1, 4, 2), (0, 4, 4))
         quantise(0, 8, 2)
         step((2, 4, 2), (1, 4, 2))
         step((1, 6, 2), (2, 4, 2))
         passes(0, 8, 2)
-        step((1, 8, 2), (1, 6, 2))
+        step((2, 6, 2), (1, 6, 2))
         turn(0, 2, 2)
         turn(2, 2, 3)
-        step((2, 6, 2), (1, 8, 2))
-        weave(0, nc.vector.tensor_copy)
-        quantise(2, 6, 2)
-        passes(2, 6, 2)
-        round_block(2, 8, 1)
+        weave(0, nc.scalar.copy)
+        weave(2, nc.scalar.copy)
+        step((1, 8, 2), (2, 6, 2))
+        step((2, 8, 1), (1, 8, 2))
         step((2, 9, 1), (2, 8, 1))
-        silu(4, 4)
-        turn(4, 2, 4)
-        weave(2, nc.vector.tensor_copy)
         quantise(2, 9, 1)
         passes(2, 9, 1)
+        silu(4, 4)
+        turn(4, 2, 4)
         silu(8, 2)
-        second_layer(0, 4, 2)
         turn(6, 2, 6)
+        h_codes = held.tile([P, S], U32, name="h_codes", tag="picked_2_8", align_bytes=64)
+        h_rounded[4] = held.tile([P, 4 * UNIT * PACK], BF16, name="h_rounded_4", tag="rounded_2_8", align_bytes=64)
+        second_layer(0, 4, 2)
         weave(4, nc.vector.tensor_copy)
         weave(6, nc.vector.tensor_copy)
         turn(8, 1, 7)
         turn(9, 1, 0)
-        second_layer(4, 4, 3)
         weave(8, nc.vector.tensor_copy)
-        weave(9, nc.vector.tensor_copy)
+        second_layer(4, 4, 3)
+        weave(9, nc.scalar.copy)
         second_layer(8, 2, 4)
         nc.scalar.copy(y_sb[:, slots(0, 4)], results[0][:])
         nc.scalar.copy(y_sb[:, slots(4, 4)], results[4][:])
@@ -285,7 +282,11 @@ def tile_moe_pre_mlp_silu_kernel(
 
         for lo, n in OUT_PIECES:
             one = held.tile([P, n], F32, name=f"one_{lo}")
-            nc.scalar.activation(one[:], y_sb[:].indirect(pos1_sb[:, entries(lo, lo + n)]), COPY)
+            first = y_sb[:].indirect(pos1_sb[:, entries(lo, lo + n)])
+            if lo == 0:
+                nc.vector.tensor_copy(one[:], first)
+            else:
+                nc.scalar.activation(one[:], first, COPY)
             both = held.tile([P, n], F32, name=f"both_{lo}")
             nc.vector.tensor_tensor(both[:], y_sb[:].indirect(pos2_sb[:, entries(lo, lo + n)]), one[:], ADD)
             nc.sync.dma_start(out[:, lo : lo + n], both[:])

@@ -13,10 +13,11 @@ UNITS = S // UNIT
 PER_COLUMN = 16
 SPARE = 16
 
+HEAD = 3
 GATED = 10
 GATE_CUTS = [0, 192, 512, 1024, S]
 SUM_BANK = [0, 1, 2, 3, 4, 5, 6, 7, 0, 1]
-REUSE = {(0, 8): "rounded_2_0", (1, 4): "picked_2_0", (2, 4): "rounded_1_0", (1, 6): "rounded_2_2", (1, 8): "rounded_1_4"}
+REUSE = {(1, 4): "picked_2_0", (2, 4): "rounded_1_0", (1, 6): "rounded_2_2", (1, 8): "rounded_1_4"}
 OUT_PIECES = [(0, 128), (128, 320), (448, 192)]
 
 FLOPS = 2 * S * (K * H + H * N)
@@ -67,7 +68,6 @@ def tile_moe_pre_mlp_silu_kernel(
         w1_scale_sb = held.tile([P, E * PASSES, H], U8, name="w1_scale_sb", align_bytes=64)
         w2_scale_sb = held.tile([P, E, N], U8, name="w2_scale_sb", align_bytes=64)
         ident = held.tile([P, P], F32, name="ident")
-        y_sb = held.tile([P, S], F32, name="y_sb")
 
         warm = held.tile([P, 2], F32, name="warm")
         nc.vector.memset(warm[:, 0:1], 0.0)
@@ -98,11 +98,14 @@ def tile_moe_pre_mlp_silu_kernel(
         load_plane(1, 0)
         nc.sync.dma_start(offs_sb[:], offs)
         load_plane(0, 0)
-        for piece in range(4):
+        for piece in range(3):
             load_gate(piece)
-        for t in range(1, PACK):
-            load_plane(0, t)
+        load_plane(1, 1)
+        load_gate(3)
+        load_plane(0, 1)
+        for t in range(2, PACK):
             load_plane(1, t)
+            load_plane(0, t)
         for t in range(PACK):
             load_plane(2, t)
         load_scales(w1_scale_sb, w1_scales)
@@ -139,7 +142,7 @@ def tile_moe_pre_mlp_silu_kernel(
             for t in range(PACK):
                 gather_plain(s, t, first, units)
 
-        def round_block(s, first, units):
+        def round_block(s, first, units, copy=nc.vector.tensor_copy):
             values[s, first] = held.tile(
                 [P, units * UNIT, PACK], BF16, name=f"rounded_{s}_{first}", tag=REUSE.get((s, first), ""), align_bytes=64
             )
@@ -149,7 +152,7 @@ def tile_moe_pre_mlp_silu_kernel(
             rows = values[s, first][:].rearrange("p (c i) t -> p c t i", i=near)
             planes = planes_of(s, cols).rearrange("p t (c i) -> p c t i", i=near)
             if gated:
-                nc.vector.tensor_copy(rows, planes)
+                copy(rows, planes)
             else:
                 weights = gate_sb[:, cols].rearrange("p (c i) -> p c i", i=near).unsqueeze(2)
                 nc.vector.tensor_tensor(rows, planes, weights.to_broadcast([P, units * UNIT // near, PACK, near]), MULT)
@@ -229,21 +232,25 @@ def tile_moe_pre_mlp_silu_kernel(
         run(0, 4, 4)
         run(0, 8, 2)
         run(1, 0, UNITS)
+        head = slots(UNITS - HEAD, HEAD)
+        tokens = plane[1, 0][:].indirect(offs_sb[:, entries(head.start, head.stop)])
+        nc.vector.tensor_copy(picked[1, 0][:, 0, head], tokens)
         for t in range(PACK):
             ends = GATE_CUTS if t == 0 else [0, 512, 1024, S]
             for lo, hi in zip(ends, ends[1:]):
                 gather_gated(t, lo, hi)
-            gather_plain(1, t, 0, UNITS)
+            gather_plain(1, t, 0, UNITS - HEAD if t == 0 else UNITS)
         gather_run(2, 0, 4)
 
         round_block(0, 0, 4)
-        gather_run(2, 4, 2, "picked_0_0")
+        gather_run(2, 4, 4, "picked_0_0")
         step((1, 0, 4), (0, 0, 4))
-        gather_run(2, 6, 2, "rounded_0_0")
         step((0, 4, 4), (1, 0, 4))
         round_block(2, 0, 2)
         step((2, 2, 2), (2, 0, 2))
-        step((0, 8, 2), (2, 2, 2))
+        round_block(0, 8, 2, nc.scalar.copy)
+        quantise(2, 2, 2)
+        passes(2, 2, 2)
         silu(0, 4)
         gather_run(2, 8, 2, "x_codes_2_2")
         step((1, 4, 2), (0, 4, 4))
@@ -263,19 +270,20 @@ def tile_moe_pre_mlp_silu_kernel(
         passes(2, 9, 1)
         silu(4, 4)
         turn(4, 2, 4)
+        h_rounded[4] = held.tile([P, 4 * UNIT * PACK], BF16, name="h_rounded_4", align_bytes=64)
+        weave(4, nc.scalar.copy)
         silu(8, 2)
         turn(6, 2, 6)
         h_codes = held.tile([P, S], U32, name="h_codes", tag="picked_2_8", align_bytes=64)
-        h_rounded[4] = held.tile([P, 4 * UNIT * PACK], BF16, name="h_rounded_4", tag="rounded_2_8", align_bytes=64)
         second_layer(0, 4, 2)
-        weave(4, nc.vector.tensor_copy)
         weave(6, nc.vector.tensor_copy)
         turn(8, 1, 7)
         turn(9, 1, 0)
-        weave(8, nc.vector.tensor_copy)
         second_layer(4, 4, 3)
+        weave(8, nc.scalar.copy)
         weave(9, nc.scalar.copy)
         second_layer(8, 2, 4)
+        y_sb = held.tile([P, S], F32, name="y_sb", tag="hidden_9", align_bytes=64)
         nc.scalar.copy(y_sb[:, slots(0, 4)], results[0][:])
         nc.scalar.copy(y_sb[:, slots(4, 4)], results[4][:])
         nc.vector.tensor_copy(y_sb[:, slots(8, 2)], results[8][:])

@@ -17,7 +17,7 @@ HEAD = 3
 GATED = 10
 GATE_CUTS = [0, 192, 512, 1024, S]
 SUM_BANK = [0, 1, 2, 3, 4, 5, 6, 7, 0, 1]
-REUSE = {(1, 4): "picked_2_0", (2, 4): "rounded_1_0", (1, 6): "rounded_2_2", (1, 8): "rounded_1_4"}
+REUSE = {(0, 6): "rounded_1_0", (0, 4): "rounded_2_2", (1, 4): "rounded_2_0", (2, 4): "picked_2_0", (1, 6): "rounded_1_0", (1, 8): "rounded_2_0"}
 OUT_PIECES = [(0, 128), (128, 320), (448, 192)]
 
 FLOPS = 2 * S * (K * H + H * N)
@@ -142,24 +142,39 @@ def tile_moe_pre_mlp_silu_kernel(
             for t in range(PACK):
                 gather_plain(s, t, first, units)
 
-        def round_block(s, first, units, copy=nc.vector.tensor_copy):
+        def room(s, first, units):
             values[s, first] = held.tile(
                 [P, units * UNIT, PACK], BF16, name=f"rounded_{s}_{first}", tag=REUSE.get((s, first), ""), align_bytes=64
             )
+
+        def round_block(s, first, units, engine="vector", into=None):
+            if into is None:
+                room(s, first, units)
+                into = first
+            target = values[s, into][:, slots(first - into, units), :]
             cols = slots(first, units)
             gated = s == 0 and first < GATED
             near = 4 if gated else 2
-            rows = values[s, first][:].rearrange("p (c i) t -> p c t i", i=near)
+            rows = target.rearrange("p (c i) t -> p c t i", i=near)
             planes = planes_of(s, cols).rearrange("p t (c i) -> p c t i", i=near)
-            if gated:
-                copy(rows, planes)
+            if engine == "gpsimd":
+                across = planes_of(s, cols).rearrange("p t c -> p c t")
+                nc.gpsimd.tensor_scalar(target, across, 1.0, 0.0, MULT, ADD)
+            elif gated:
+                nc.vector.tensor_copy(rows, planes)
             else:
-                weights = gate_sb[:, cols].rearrange("p (c i) -> p c i", i=near).unsqueeze(2)
+                if first < 6:
+                    base = 0 if first < 4 else 4
+                    source = gate_psum[base][:, slots(first - base, units)]
+                else:
+                    source = gate_sb[:, cols]
+                weights = source.rearrange("p (c i) -> p c i", i=near).unsqueeze(2)
                 nc.vector.tensor_tensor(rows, planes, weights.to_broadcast([P, units * UNIT // near, PACK, near]), MULT)
 
         def quantise(s, first, units):
             count = units * UNIT
-            codes = held.tile([P, count], U32, name=f"x_codes_{s}_{first}", align_bytes=64)
+            tag = "picked_0_8" if (s, first) == (0, 8) else ""
+            codes = held.tile([P, count], U32, name=f"x_codes_{s}_{first}", tag=tag, align_bytes=64)
             scales = held.tile([P, count], U8, name=f"x_scales_{s}_{first}", align_bytes=64)
             nc.vector.quantize_mx(
                 codes[:].bitcast(FP8X4), scales[:], values[s, first][:].rearrange("p c t -> p (c t)")
@@ -228,7 +243,23 @@ def tile_moe_pre_mlp_silu_kernel(
                     stop=True,
                 )
 
-        run(0, 0, 4)
+        def gate_into_psum():
+            gate_column = held.tile([P, 6], F32, name="gate_column")
+            for first, units, bank in [(0, 4, 6), (4, 2, 7)]:
+                across = psum.tile([P, units, UNIT], F32, name=f"gate_turned_{first}", tag=f"bank_{bank}")
+                for u in range(units):
+                    nc.tensor.transpose(across[:, u, :], gate_sb[:, slots(first + u, 1)], ident[:])
+                nc.vector.tensor_copy(gate_column[:, first : first + units], across[:, :, 0])
+            for first, units, bank in [(0, 4, 4), (4, 2, 5)]:
+                spread = psum.tile([P, units * UNIT], F32, name=f"gate_psum_{first}", tag=f"bank_{bank}")
+                for u in range(units):
+                    column = gate_column[:, first + u : first + u + 1].to_broadcast([P, P])
+                    nc.tensor.transpose(spread[:, slots(u, 1)], column, ident[:])
+                gate_psum[first] = spread
+
+        gate_psum = {}
+        shared = ctx.enter_context(tc.tile_pool(name="shared", bufs=1))
+        picked[0, 0] = shared.tile([P, PACK, 4 * UNIT], F32, name="picked_0_0", align_bytes=64, offset=0)
         run(0, 4, 4)
         run(0, 8, 2)
         run(1, 0, UNITS)
@@ -240,24 +271,36 @@ def tile_moe_pre_mlp_silu_kernel(
             for lo, hi in zip(ends, ends[1:]):
                 gather_gated(t, lo, hi)
             gather_plain(1, t, 0, UNITS - HEAD if t == 0 else UNITS)
+            if t == 1:
+                gate_into_psum()
         gather_run(2, 0, 4)
 
         round_block(0, 0, 4)
-        gather_run(2, 4, 4, "picked_0_0")
+        values[0, 8] = shared.tile([P, 2 * UNIT, PACK], BF16, name="rounded_0_8", align_bytes=64, offset=0)
+        round_block(0, 8, 2, "gpsimd", 8)
+        picked[2, 4] = shared.tile([P, PACK, 4 * UNIT], F32, name="picked_2_4", align_bytes=64, offset=4096)
+        for t in range(PACK):
+            gather_plain(2, t, 4, 4)
         step((1, 0, 4), (0, 0, 4))
-        step((0, 4, 4), (1, 0, 4))
+        quantise(1, 0, 4)
+        passes(1, 0, 4)
+        round_block(0, 6, 2, "gpsimd")
         round_block(2, 0, 2)
         step((2, 2, 2), (2, 0, 2))
-        round_block(0, 8, 2, nc.scalar.copy)
+        quantise(0, 6, 2)
         quantise(2, 2, 2)
         passes(2, 2, 2)
+        passes(0, 6, 2)
+        round_block(0, 4, 2, "gpsimd")
         silu(0, 4)
         gather_run(2, 8, 2, "x_codes_2_2")
-        step((1, 4, 2), (0, 4, 4))
-        quantise(0, 8, 2)
-        step((2, 4, 2), (1, 4, 2))
+        round_block(1, 4, 2)
+        step((2, 4, 2), (0, 8, 2))
+        quantise(0, 4, 2)
+        passes(0, 4, 2)
+        quantise(1, 4, 2)
+        passes(1, 4, 2)
         step((1, 6, 2), (2, 4, 2))
-        passes(0, 8, 2)
         step((2, 6, 2), (1, 6, 2))
         turn(0, 2, 2)
         turn(2, 2, 3)

@@ -17,7 +17,7 @@ HEAD = 3
 GATED = 10
 GATE_CUTS = [0, 192, 512, 1024, S]
 SUM_BANK = [0, 1, 2, 3, 4, 5, 6, 7, 0, 1]
-REUSE = {(0, 6): "rounded_1_0", (0, 4): "rounded_2_2", (1, 4): "rounded_2_0", (2, 4): "picked_2_0", (1, 6): "rounded_1_0", (1, 8): "rounded_2_0"}
+REUSE = {(0, 6): "rounded_1_0", (0, 4): "rounded_0_0", (1, 9): "rounded_2_2", (1, 4): "rounded_2_0", (2, 4): "picked_2_0", (1, 6): "rounded_1_0", (1, 8): "rounded_2_0"}
 OUT_PIECES = [(0, 128), (128, 320), (448, 192)]
 
 FLOPS = 2 * S * (K * H + H * N)
@@ -159,7 +159,13 @@ def tile_moe_pre_mlp_silu_kernel(
             planes = planes_of(s, cols).rearrange("p t (c i) -> p c t i", i=near)
             if engine == "gpsimd":
                 across = planes_of(s, cols).rearrange("p t c -> p c t")
-                nc.gpsimd.tensor_scalar(target, across, 1.0, 0.0, MULT, ADD)
+                if gated:
+                    nc.gpsimd.tensor_scalar(target, across, 1.0, 0.0, MULT, ADD)
+                else:
+                    weights = gate_sb[:, cols].unsqueeze(2).to_broadcast([P, units * UNIT, PACK])
+                    nc.gpsimd.tensor_tensor(target, across, weights, MULT)
+            elif engine == "scalar":
+                nc.scalar.copy(rows, planes)
             elif gated:
                 nc.vector.tensor_copy(rows, planes)
             else:
@@ -232,13 +238,14 @@ def tile_moe_pre_mlp_silu_kernel(
             cols = slots(first, units)
             nc.vector.quantize_mx(h_codes[:, cols].bitcast(FP8X4), h_scales[:, cols], h_rows(first, units))
             results[first] = psum.tile([P, units * UNIT], F32, name=f"results_{first}", tag=f"bank_{bank}")
-            for a in range(cols.start, cols.stop, C):
+            wide = min(C, units * UNIT)
+            for a in range(cols.start, cols.stop, wide):
                 nc.tensor.matmul_mx(
-                    out=results[first][:, a - cols.start : a - cols.start + C],
+                    out=results[first][:, a - cols.start : a - cols.start + wide],
                     lhsT=w2_sb[:, a // C, :].bitcast(FP4X4),
                     lhsT_scale=w2_scale_sb[:, a // C, :],
-                    rhs=h_codes[:, a : a + C].bitcast(FP8X4),
-                    rhs_scale=h_scales[:, a : a + C],
+                    rhs=h_codes[:, a : a + wide].bitcast(FP8X4),
+                    rhs_scale=h_scales[:, a : a + wide],
                     start=True,
                     stop=True,
                 )
@@ -282,6 +289,7 @@ def tile_moe_pre_mlp_silu_kernel(
         for t in range(PACK):
             gather_plain(2, t, 4, 4)
         step((1, 0, 4), (0, 0, 4))
+        round_block(0, 4, 2, "scalar")
         quantise(1, 0, 4)
         passes(1, 0, 4)
         round_block(0, 6, 2, "gpsimd")
@@ -291,7 +299,7 @@ def tile_moe_pre_mlp_silu_kernel(
         quantise(2, 2, 2)
         passes(2, 2, 2)
         passes(0, 6, 2)
-        round_block(0, 4, 2, "gpsimd")
+        round_block(1, 9, 1, "gpsimd")
         silu(0, 4)
         gather_run(2, 8, 2, "x_codes_2_2")
         round_block(1, 4, 2)
@@ -306,30 +314,34 @@ def tile_moe_pre_mlp_silu_kernel(
         turn(2, 2, 3)
         weave(0, nc.scalar.copy)
         weave(2, nc.scalar.copy)
-        step((1, 8, 2), (2, 6, 2))
-        step((2, 8, 1), (1, 8, 2))
+        step((1, 8, 1), (1, 9, 1))
+        quantise(2, 6, 2)
+        passes(2, 6, 2)
+        step((2, 8, 1), (1, 8, 1))
         step((2, 9, 1), (2, 8, 1))
         quantise(2, 9, 1)
         passes(2, 9, 1)
         silu(4, 4)
         turn(4, 2, 4)
-        h_rounded[4] = held.tile([P, 4 * UNIT * PACK], BF16, name="h_rounded_4", align_bytes=64)
-        weave(4, nc.scalar.copy)
+        h_rounded[4] = held.tile([P, 4 * UNIT * PACK], BF16, name="h_rounded_4", tag="rounded_2_8", align_bytes=64)
         silu(8, 2)
         turn(6, 2, 6)
         h_codes = held.tile([P, S], U32, name="h_codes", tag="picked_2_8", align_bytes=64)
         second_layer(0, 4, 2)
+        weave(4, nc.vector.tensor_copy)
         weave(6, nc.vector.tensor_copy)
         turn(8, 1, 7)
         turn(9, 1, 0)
         second_layer(4, 4, 3)
         weave(8, nc.scalar.copy)
         weave(9, nc.scalar.copy)
-        second_layer(8, 2, 4)
+        second_layer(8, 1, 4)
+        second_layer(9, 1, 1)
         y_sb = held.tile([P, S], F32, name="y_sb", tag="hidden_9", align_bytes=64)
         nc.scalar.copy(y_sb[:, slots(0, 4)], results[0][:])
         nc.scalar.copy(y_sb[:, slots(4, 4)], results[4][:])
-        nc.vector.tensor_copy(y_sb[:, slots(8, 2)], results[8][:])
+        nc.vector.tensor_copy(y_sb[:, slots(8, 1)], results[8][:])
+        nc.vector.tensor_copy(y_sb[:, slots(9, 1)], results[9][:])
 
         for lo, n in OUT_PIECES:
             one = held.tile([P, n], F32, name=f"one_{lo}")

@@ -17,7 +17,7 @@ HEAD = 3
 GATED = 10
 GATE_CUTS = [0, 192, 512, 1024, S]
 SUM_BANK = [0, 1, 2, 3, 4, 5, 6, 7, 0, 1]
-REUSE = {(0, 6): "rounded_1_0", (0, 4): "rounded_0_0", (1, 9): "rounded_2_2", (1, 4): "rounded_2_0", (2, 4): "picked_2_0", (1, 6): "rounded_1_0", (1, 8): "rounded_2_0"}
+REUSE = {(0, 6): "rounded_1_0", (0, 4): "rounded_0_0", (1, 8): "rounded_2_2", (1, 4): "rounded_2_0", (2, 4): "picked_2_0", (1, 6): "rounded_1_0", (2, 6): "rounded_2_0"}
 OUT_PIECES = [(0, 128), (128, 320), (448, 192)]
 
 FLOPS = 2 * S * (K * H + H * N)
@@ -169,7 +169,7 @@ def tile_moe_pre_mlp_silu_kernel(
             elif gated:
                 nc.vector.tensor_copy(rows, planes)
             else:
-                if first < 6:
+                if first < 6 or (s, first) == (1, 6):
                     base = 0 if first < 4 else 4
                     source = gate_psum[base][:, slots(first - base, units)]
                 else:
@@ -251,13 +251,13 @@ def tile_moe_pre_mlp_silu_kernel(
                 )
 
         def gate_into_psum():
-            gate_column = held.tile([P, 6], F32, name="gate_column")
-            for first, units, bank in [(0, 4, 6), (4, 2, 7)]:
+            gate_column = held.tile([P, 8], F32, name="gate_column")
+            for first, units, bank in [(0, 4, 6), (4, 4, 7)]:
                 across = psum.tile([P, units, UNIT], F32, name=f"gate_turned_{first}", tag=f"bank_{bank}")
                 for u in range(units):
                     nc.tensor.transpose(across[:, u, :], gate_sb[:, slots(first + u, 1)], ident[:])
                 nc.vector.tensor_copy(gate_column[:, first : first + units], across[:, :, 0])
-            for first, units, bank in [(0, 4, 4), (4, 2, 5)]:
+            for first, units, bank in [(0, 4, 4), (4, 4, 5)]:
                 spread = psum.tile([P, units * UNIT], F32, name=f"gate_psum_{first}", tag=f"bank_{bank}")
                 for u in range(units):
                     column = gate_column[:, first + u : first + u + 1].to_broadcast([P, P])
@@ -296,50 +296,53 @@ def tile_moe_pre_mlp_silu_kernel(
         round_block(2, 0, 2)
         step((2, 2, 2), (2, 0, 2))
         quantise(0, 6, 2)
+        quantise(0, 8, 2)
         quantise(2, 2, 2)
         passes(2, 2, 2)
         passes(0, 6, 2)
-        round_block(1, 9, 1, "gpsimd")
+        round_block(1, 8, 2, "gpsimd")
         silu(0, 4)
         gather_run(2, 8, 2, "x_codes_2_2")
+        passes(0, 8, 2)
         round_block(1, 4, 2)
-        step((2, 4, 2), (0, 8, 2))
-        quantise(0, 4, 2)
-        passes(0, 4, 2)
-        quantise(1, 4, 2)
-        passes(1, 4, 2)
-        step((1, 6, 2), (2, 4, 2))
+        round_block(2, 4, 2)
+        round_block(1, 6, 2)
+        for s in range(PASSES):
+            quantise(s, 4, 2)
+            passes(s, 4, 2)
         step((2, 6, 2), (1, 6, 2))
         turn(0, 2, 2)
         turn(2, 2, 3)
         weave(0, nc.scalar.copy)
-        weave(2, nc.scalar.copy)
-        step((1, 8, 1), (1, 9, 1))
         quantise(2, 6, 2)
         passes(2, 6, 2)
-        step((2, 8, 1), (1, 8, 1))
+        weave(2, nc.vector.tensor_copy)
+        step((2, 8, 1), (1, 8, 2))
         step((2, 9, 1), (2, 8, 1))
         quantise(2, 9, 1)
         passes(2, 9, 1)
         silu(4, 4)
         turn(4, 2, 4)
-        h_rounded[4] = held.tile([P, 4 * UNIT * PACK], BF16, name="h_rounded_4", tag="rounded_2_8", align_bytes=64)
+        h_rounded[4] = held.tile([P, 2 * UNIT * PACK], BF16, name="h_rounded_4", tag="rounded_2_8", align_bytes=64)
+        h_rounded[6] = held.tile([P, 2 * UNIT * PACK], BF16, name="h_rounded_6", align_bytes=64)
         silu(8, 2)
         turn(6, 2, 6)
         h_codes = held.tile([P, S], U32, name="h_codes", tag="picked_2_8", align_bytes=64)
         second_layer(0, 4, 2)
         weave(4, nc.vector.tensor_copy)
+        second_layer(4, 2, 3)
         weave(6, nc.vector.tensor_copy)
         turn(8, 1, 7)
         turn(9, 1, 0)
-        second_layer(4, 4, 3)
+        second_layer(6, 2, 5)
         weave(8, nc.scalar.copy)
         weave(9, nc.scalar.copy)
         second_layer(8, 1, 4)
         second_layer(9, 1, 1)
         y_sb = held.tile([P, S], F32, name="y_sb", tag="hidden_9", align_bytes=64)
         nc.scalar.copy(y_sb[:, slots(0, 4)], results[0][:])
-        nc.scalar.copy(y_sb[:, slots(4, 4)], results[4][:])
+        nc.scalar.copy(y_sb[:, slots(4, 2)], results[4][:])
+        nc.vector.tensor_copy(y_sb[:, slots(6, 2)], results[6][:])
         nc.vector.tensor_copy(y_sb[:, slots(8, 1)], results[8][:])
         nc.vector.tensor_copy(y_sb[:, slots(9, 1)], results[9][:])
 

from contextlib import ExitStack

import concourse.mybir as mybir
from concourse.masks import make_identity

K, T, E, C, H, N = 1536, 640, 5, 256, 512, 128
S = E * C
P = 128
PACK = 4
PASSES = K // (P * PACK)
UNIT = 128
UNITS = S // UNIT
PER_COLUMN = 16
SPARE = 16

HEAD = 3
GATED = 10
GATE_CUTS = [0, 192, 512, 1024, S]
SUM_BANK = [0, 1, 2, 3, 4, 5, 6, 7, 0, 1]
REUSE = {(0, 6): "rounded_1_0", (0, 4): "rounded_0_0", (1, 8): "rounded_2_2", (1, 4): "rounded_2_0", (2, 4): "picked_2_0", (1, 6): "rounded_1_0", (2, 6): "rounded_2_0"}
OUT_PIECES = [(0, 128), (128, 320), (448, 192)]

FLOPS = 2 * S * (K * H + H * N)
BYTES = 4 * K * T + E * (K * H + H * N) // 2 + E * (K * H + H * N) // 32 + 4 * S + 2 * P * (S + 2 * T) // 16 + 4 * N * T

F32 = mybir.dt.float32
BF16 = mybir.dt.bfloat16
I32 = mybir.dt.int32
U32 = mybir.dt.uint32
U16 = mybir.dt.uint16
U8 = mybir.dt.uint8
FP8X4 = mybir.dt.float8_e4m3fn_x4
FP4X4 = mybir.dt.float4_e2m1fn_x4
MULT = mybir.AluOpType.mult
ADD = mybir.AluOpType.add
SILU = mybir.ActivationFunctionType.Silu
COPY = mybir.ActivationFunctionType.Copy


def slots(first, units):
    return slice(first * UNIT, (first + units) * UNIT)


def entries(lo, hi):
    return slice(lo // PER_COLUMN, hi // PER_COLUMN)


def tile_moe_pre_mlp_silu_kernel(
    tc, xT, w1_words, w1_scales, w2_words, w2_scales, gate, offs, pos1, pos2, out
):
    nc = tc.nc
    with ExitStack() as ctx:
        held = ctx.enter_context(tc.tile_pool(name="held", bufs=1))
        psum = ctx.enter_context(tc.psum_pool(name="psum", bufs=1))

        offs_sb = held.tile([P, S // PER_COLUMN], U16, name="offs_sb")
        pos1_sb = held.tile([P, T // PER_COLUMN], U16, name="pos1_sb")
        pos2_sb = held.tile([P, T // PER_COLUMN], U16, name="pos2_sb")
        width = [T, SPARE + S, T]
        plane = {
            (s, t): held.tile([P, width[s]], F32, name=f"plane_{s}_{t}", align_bytes=64)
            for s in range(PASSES)
            for t in range(PACK)
        }
        gate_sb = held.tile([P, S], F32, name="gate_sb", align_bytes=64)
        w1_sb = [held.tile([P, PASSES, 2 * H], U8, name=f"w1_{e}", align_bytes=64) for e in range(E)]
        w2_sb = held.tile([P, E, 2 * N], U8, name="w2_sb", align_bytes=64)
        w1_scale_sb = held.tile([P, E * PASSES, H], U8, name="w1_scale_sb", align_bytes=64)
        w2_scale_sb = held.tile([P, E, N], U8, name="w2_scale_sb", align_bytes=64)
        ident = held.tile([P, P], F32, name="ident")

        warm = held.tile([P, 2], F32, name="warm")
        nc.vector.memset(warm[:, 0:1], 0.0)
        nc.scalar.activation(warm[:, 1:2], warm[:, 0:1], SILU)
        nc.vector.memset(w1_scale_sb[:].rearrange("p a i -> p (a i)").bitcast(I32), 0)
        nc.vector.memset(w2_scale_sb[:].rearrange("p a i -> p (a i)").bitcast(I32), 0)
        for t in range(PACK):
            nc.gpsimd.memset(plane[1, t][:, T:], 0.0)
        make_identity(nc, ident[:])

        x_rows = xT.rearrange("(s p t) c -> s t p c", p=P, t=PACK)

        def load_plane(s, t):
            nc.sync.dma_start(plane[s, t][:, 0:T], x_rows[s, t])

        def load_gate(piece):
            cols = slice(GATE_CUTS[piece], GATE_CUTS[piece + 1])
            nc.sync.dma_start(gate_sb[:, cols], gate[0:P, cols])

        def load_scales(scale_sb, scales):
            rows = scales.rearrange("e s (q r) i -> r q (e s) i", r=4).bitcast(I32)
            for r in range(4):
                nc.sync.dma_start(scale_sb[r:P:32].bitcast(I32), rows[r])

        def load_w1(e):
            nc.sync.dma_start(w1_sb[e][:].bitcast(I32), w1_words[e].rearrange("s p b -> p s b").bitcast(I32))

        load_plane(1, 0)
        nc.sync.dma_start(offs_sb[:], offs)
        load_plane(0, 0)
        for piece in range(3):
            load_gate(piece)
        load_plane(1, 1)
        load_gate(3)
        load_plane(0, 1)
        for t in range(2, PACK):
            load_plane(1, t)
            load_plane(0, t)
        for t in range(PACK):
            load_plane(2, t)
        load_scales(w1_scale_sb, w1_scales)
        for e in range(E):
            load_w1(e)
        nc.sync.dma_start(w2_sb[:].bitcast(I32), w2_words.rearrange("e s p b -> p (e s) b").bitcast(I32))
        load_scales(w2_scale_sb, w2_scales)
        nc.sync.dma_start(pos1_sb[:], pos1)
        nc.sync.dma_start(pos2_sb[:], pos2)

        h_scales = held.tile([P, S], U8, name="h_scales", align_bytes=64)
        picked, values, operand, sums, hidden, turned, h_rounded, results = {}, {}, {}, {}, {}, {}, {}, {}

        def run(s, first, units, tag=""):
            picked[s, first] = held.tile(
                [P, PACK, units * UNIT], F32, name=f"picked_{s}_{first}", tag=tag, align_bytes=64
            )

        def planes_of(s, cols):
            first = max(f for a, f in picked if a == s and f * UNIT <= cols.start)
            return picked[s, first][:, :, cols.start - first * UNIT : cols.stop - first * UNIT]

        def gather_gated(t, lo, hi):
            tokens = plane[0, t][:].indirect(offs_sb[:, entries(lo, hi)])
            nc.vector.tensor_tensor(planes_of(0, slice(lo, hi))[:, t, :], tokens, gate_sb[:, lo:hi], MULT)

        def gather_plain(s, t, first, units):
            cols = slots(first, units)
            tokens = plane[s, t][:].indirect(offs_sb[:, entries(cols.start, cols.stop)])
            nc.scalar.activation(planes_of(s, cols)[:, t, :], tokens, COPY)

        def gather_run(s, first, units, tag=""):
            run(s, first, units, tag)
            for t in range(PACK):
                gather_plain(s, t, first, units)

        def room(s, first, units):
            values[s, first] = held.tile(
                [P, units * UNIT, PACK], BF16, name=f"rounded_{s}_{first}", tag=REUSE.get((s, first), ""), align_bytes=64
            )

        def round_block(s, first, units, engine="vector", into=None):
            if into is None:
                room(s, first, units)
                into = first
            target = values[s, into][:, slots(first - into, units), :]
            cols = slots(first, units)
            gated = s == 0 and first < GATED
            near = 4 if gated else 2
            rows = target.rearrange("p (c i) t -> p c t i", i=near)
            planes = planes_of(s, cols).rearrange("p t (c i) -> p c t i", i=near)
            if engine == "gpsimd":
                across = planes_of(s, cols).rearrange("p t c -> p c t")
                if gated:
                    nc.gpsimd.tensor_scalar(target, across, 1.0, 0.0, MULT, ADD)
                else:
                    weights = gate_sb[:, cols].unsqueeze(2).to_broadcast([P, units * UNIT, PACK])
                    nc.gpsimd.tensor_tensor(target, across, weights, MULT)
            elif engine == "scalar":
                nc.scalar.copy(rows, planes)
            elif gated:
                nc.vector.tensor_copy(rows, planes)
            else:
                if first < 6 or (s, first) == (1, 6):
                    base = 0 if first < 4 else 4
                    source = gate_psum[base][:, slots(first - base, units)]
                else:
                    source = gate_sb[:, cols]
                weights = source.rearrange("p (c i) -> p c i", i=near).unsqueeze(2)
                nc.vector.tensor_tensor(rows, planes, weights.to_broadcast([P, units * UNIT // near, PACK, near]), MULT)

        def quantise(s, first, units):
            count = units * UNIT
            tag = "picked_0_8" if (s, first) == (0, 8) else ""
            codes = held.tile([P, count], U32, name=f"x_codes_{s}_{first}", tag=tag, align_bytes=64)
            scales = held.tile([P, count], U8, name=f"x_scales_{s}_{first}", align_bytes=64)
            nc.vector.quantize_mx(
                codes[:].bitcast(FP8X4), scales[:], values[s, first][:].rearrange("p c t -> p (c t)")
            )
            for b in range(units):
                operand[first + b, s] = codes[:, slots(b, 1)], scales[:, slots(b, 1)]

        def passes(s, first, units):
            for u in range(first, first + units):
                e = u * UNIT // C
                if s == 0:
                    sums[u] = psum.tile([P, H], F32, name=f"sums_{u}", tag=f"bank_{SUM_BANK[u]}")
                codes, scales = operand[u, s]
                nc.tensor.matmul_mx(
                    out=sums[u][:],
                    lhsT=codes.bitcast(FP8X4),
                    lhsT_scale=scales,
                    rhs=w1_sb[e][:, s, :].bitcast(FP4X4),
                    rhs_scale=w1_scale_sb[:, e * PASSES + s, :],
                    start=(s == 0),
                    stop=(s == PASSES - 1),
                )

        def step(block, before):
            round_block(*block)
            quantise(*before)
            passes(*before)

        def silu(first, units):
            for u in range(first, first + units):
                by_half = sums[u][:].rearrange("c (p v d) -> c v p d", v=2, d=2)
                hidden[u] = held.tile([P, 2, P, 2], BF16, name=f"hidden_{u}", align_bytes=64)
                nc.scalar.activation(hidden[u][:], by_half, SILU)

        def turn(first, units, bank):
            turned[first] = psum.tile([P, units, 2, UNIT], F32, name=f"turned_{first}", tag=f"bank_{bank}")
            for u in range(first, first + units):
                for v in range(2):
                    pairs = hidden[u][:, v].rearrange("c p d -> c (p d)").bitcast(F32)
                    nc.tensor.transpose(turned[first][:, u - first, v, :], pairs, ident[:])

        for first, units in [(0, 4), (8, 2)]:
            h_rounded[first] = held.tile([P, units * UNIT * PACK], BF16, name=f"h_rounded_{first}", align_bytes=64)

        def h_rows(first, units):
            base = max(f for f in h_rounded if f <= first)
            return h_rounded[base][:, (first - base) * UNIT * PACK : (first - base + units) * UNIT * PACK]

        def weave(first, copy):
            units = turned[first].shape[1]
            words = h_rows(first, units).bitcast(F32).rearrange("p (u c v) -> p u c v", u=units, v=2)
            copy(words, turned[first][:].rearrange("p u v c -> p u c v"))

        def second_layer(first, units, bank):
            cols = slots(first, units)
            nc.vector.quantize_mx(h_codes[:, cols].bitcast(FP8X4), h_scales[:, cols], h_rows(first, units))
            results[first] = psum.tile([P, units * UNIT], F32, name=f"results_{first}", tag=f"bank_{bank}")
            wide = min(C, units * UNIT)
            for a in range(cols.start, cols.stop, wide):
                nc.tensor.matmul_mx(
                    out=results[first][:, a - cols.start : a - cols.start + wide],
                    lhsT=w2_sb[:, a // C, :].bitcast(FP4X4),
                    lhsT_scale=w2_scale_sb[:, a // C, :],
                    rhs=h_codes[:, a : a + wide].bitcast(FP8X4),
                    rhs_scale=h_scales[:, a : a + wide],
                    start=True,
                    stop=True,
                )

        def gate_into_psum():
            gate_column = held.tile([P, 8], F32, name="gate_column")
            for first, units, bank in [(0, 4, 6), (4, 4, 7)]:
                across = psum.tile([P, units, UNIT], F32, name=f"gate_turned_{first}", tag=f"bank_{bank}")
                for u in range(units):
                    nc.tensor.transpose(across[:, u, :], gate_sb[:, slots(first + u, 1)], ident[:])
                nc.vector.tensor_copy(gate_column[:, first : first + units], across[:, :, 0])
            for first, units, bank in [(0, 4, 4), (4, 4, 5)]:
                spread = psum.tile([P, units * UNIT], F32, name=f"gate_psum_{first}", tag=f"bank_{bank}")
                for u in range(units):
                    column = gate_column[:, first + u : first + u + 1].to_broadcast([P, P])
                    nc.tensor.transpose(spread[:, slots(u, 1)], column, ident[:])
                gate_psum[first] = spread

        gate_psum = {}
        shared = ctx.enter_context(tc.tile_pool(name="shared", bufs=1))
        picked[0, 0] = shared.tile([P, PACK, 4 * UNIT], F32, name="picked_0_0", align_bytes=64, offset=0)
        run(0, 4, 4)
        run(0, 8, 2)
        run(1, 0, UNITS)
        head = slots(UNITS - HEAD, HEAD)
        tokens = plane[1, 0][:].indirect(offs_sb[:, entries(head.start, head.stop)])
        nc.vector.tensor_copy(picked[1, 0][:, 0, head], tokens)
        for t in range(PACK):
            ends = GATE_CUTS if t == 0 else [0, 512, 1024, S]
            for lo, hi in zip(ends, ends[1:]):
                gather_gated(t, lo, hi)
            gather_plain(1, t, 0, UNITS - HEAD if t == 0 else UNITS)
            if t == 1:
                gate_into_psum()
        gather_run(2, 0, 4)

        round_block(0, 0, 4)
        values[0, 8] = shared.tile([P, 2 * UNIT, PACK], BF16, name="rounded_0_8", align_bytes=64, offset=0)
        round_block(0, 8, 2, "gpsimd", 8)
        picked[2, 4] = shared.tile([P, PACK, 4 * UNIT], F32, name="picked_2_4", align_bytes=64, offset=4096)
        for t in range(PACK):
            gather_plain(2, t, 4, 4)
        step((1, 0, 4), (0, 0, 4))
        round_block(0, 4, 2, "scalar")
        quantise(1, 0, 4)
        passes(1, 0, 4)
        round_block(0, 6, 2, "gpsimd")
        round_block(2, 0, 2)
        step((2, 2, 2), (2, 0, 2))
        quantise(0, 6, 2)
        quantise(0, 8, 2)
        quantise(2, 2, 2)
        passes(2, 2, 2)
        passes(0, 6, 2)
        round_block(1, 8, 2, "gpsimd")
        silu(0, 4)
        gather_run(2, 8, 2, "x_codes_2_2")
        passes(0, 8, 2)
        round_block(1, 4, 2)
        round_block(2, 4, 2)
        round_block(1, 6, 2)
        for s in range(PASSES):
            quantise(s, 4, 2)
            passes(s, 4, 2)
        step((2, 6, 2), (1, 6, 2))
        turn(0, 2, 2)
        turn(2, 2, 3)
        weave(0, nc.scalar.copy)
        quantise(2, 6, 2)
        passes(2, 6, 2)
        weave(2, nc.vector.tensor_copy)
        step((2, 8, 1), (1, 8, 2))
        step((2, 9, 1), (2, 8, 1))
        quantise(2, 9, 1)
        passes(2, 9, 1)
        silu(4, 4)
        turn(4, 2, 4)
        h_rounded[4] = held.tile([P, 2 * UNIT * PACK], BF16, name="h_rounded_4", tag="rounded_2_8", align_bytes=64)
        h_rounded[6] = held.tile([P, 2 * UNIT * PACK], BF16, name="h_rounded_6", align_bytes=64)
        silu(8, 2)
        turn(6, 2, 6)
        h_codes = held.tile([P, S], U32, name="h_codes", tag="picked_2_8", align_bytes=64)
        second_layer(0, 4, 2)
        weave(4, nc.vector.tensor_copy)
        second_layer(4, 2, 3)
        weave(6, nc.vector.tensor_copy)
        turn(8, 1, 7)
        turn(9, 1, 0)
        second_layer(6, 2, 5)
        weave(8, nc.scalar.copy)
        weave(9, nc.scalar.copy)
        second_layer(8, 1, 4)
        second_layer(9, 1, 1)
        y_sb = held.tile([P, S], F32, name="y_sb", tag="hidden_9", align_bytes=64)
        nc.scalar.copy(y_sb[:, slots(0, 4)], results[0][:])
        nc.scalar.copy(y_sb[:, slots(4, 2)], results[4][:])
        nc.vector.tensor_copy(y_sb[:, slots(6, 2)], results[6][:])
        nc.vector.tensor_copy(y_sb[:, slots(8, 1)], results[8][:])
        nc.vector.tensor_copy(y_sb[:, slots(9, 1)], results[9][:])

        for lo, n in OUT_PIECES:
            one = held.tile([P, n], F32, name=f"one_{lo}")
            first = y_sb[:].indirect(pos1_sb[:, entries(lo, lo + n)])
            if lo == 0:
                nc.vector.tensor_copy(one[:], first)
            else:
                nc.scalar.activation(one[:], first, COPY)
            both = held.tile([P, n], F32, name=f"both_{lo}")
            nc.vector.tensor_tensor(both[:], y_sb[:].indirect(pos2_sb[:, entries(lo, lo + n)]), one[:], ADD)
            nc.sync.dma_start(out[:, lo : lo + n], both[:])
